import numpy as np
import ml_dtypes


def mxq(x, axis, fmt="e4m3"):
    dtype, down = {"e4m3": (ml_dtypes.float8_e4m3fn, 7), "e5m2": (ml_dtypes.float8_e5m2, 14)}[fmt]
    v = np.moveaxis(np.asarray(x, np.float32).astype(ml_dtypes.bfloat16).astype(np.float64), axis, -1)
    blocks = v.reshape(v.shape[:-1] + (-1, 32))
    amax = np.abs(blocks).max(-1, keepdims=True)
    byte = np.maximum(np.where(amax > 0, np.frexp(amax)[1] - 1 + 127, 0) - down, 1)
    scale = np.exp2(byte - 127.0)
    codes = (blocks / scale).astype(np.float32).astype(dtype).astype(np.float64)
    return np.moveaxis((codes * scale).reshape(v.shape), -1, axis)


WIDE = False


def mx_kscale(k):
    if not WIDE:
        return np.ones(k)
    levels = np.array([10, -10, 5, -5, 0])
    if k % 512:
        return np.exp2(np.random.permutation(np.resize(levels, k // 32))).repeat(32)
    a = np.empty((k // 512, 16))
    for p in range(k // 512):
        a[p, :8] = np.random.permutation(np.resize(levels, 8))
        for g in range(8):
            far = levels[np.abs(levels - a[p, g]) >= 10]
            a[p, g + 8] = far[np.random.randint(len(far))]
    return np.exp2(a.ravel()).repeat(32)


def f64(x):
    return np.asarray(x).astype(np.float64)


def striped(idx):
    return np.tile(idx.reshape(-1, 16).T, (8, 1)).astype(np.uint16)


def unstriped(offs):
    return offs[:16].T.reshape(-1).astype(np.int64)


def striped8(idx):
    return np.concatenate([x.reshape(-1, 16).T for x in idx]).astype(np.uint16)


def runs(offs, k):
    lists = np.stack([offs[16 * r : 16 * r + 16].T.reshape(-1) for r in range(8)]).astype(np.int64)
    return lists[np.arange(k) % 512 // 64]


def pack_weight(w):
    k, n = w.shape
    w = f64(np.asarray(w, np.float32).astype(ml_dtypes.bfloat16)).reshape(k // 32, 32, n)
    amax = np.abs(w).max(1)
    byte = np.clip(np.where(amax > 0, np.frexp(amax)[1] - 1 + 127 - 7, 1), 1, 254)
    scaled = (w * np.exp2(127.0 - byte)[:, None, :]).reshape(k, n).astype(np.float32)
    words = np.ascontiguousarray(scaled.reshape(k // 512, 128, 4, n).transpose(0, 1, 3, 2)).astype(ml_dtypes.float8_e4m3fn).view(np.uint8)
    return words, np.ascontiguousarray(byte.astype(np.uint8).reshape(k // 512, 16, n))


def unpack_weight(words, scales):
    g, p, n, _ = words.shape
    vals = np.ascontiguousarray(words).view(ml_dtypes.float8_e4m3fn).astype(np.float64) * np.repeat(np.exp2(scales.astype(np.float64) - 127.0), 8, axis=1)[..., None]
    return vals.transpose(0, 1, 3, 2).reshape(g * 512, n)


def relu(v):
    return np.maximum(v, 0.0)


K, T, S, N, H = 1024, 2048, 512, 512, 512


def setup_inputs():
    n = np.random.standard_normal
    s = mx_kscale(K)[:, None]
    u = mx_kscale(H)
    packed_xT = pack_weight(n((K, T)) * s)
    return {
        "x_words": packed_xT[0],
        "x_scales": packed_xT[1],
        "w1": (n((K, H)) / np.sqrt(K) / s * u).astype(np.float32),
        "w2": (n((K, H)) / np.sqrt(K) / s).astype(np.float32),
        "w3": (n((H, N)) / np.sqrt(H) / u[:, None]).astype(np.float32),
        "offs": striped(np.random.permutation(T)[:S]),
        "east": striped8(np.stack([np.random.permutation(S) for _ in range(8)])),
        "west": striped8(np.stack([np.random.permutation(S) for _ in range(8)])),
    }


def reference(x_words, x_scales, w1, w2, w3, offs, east, west):
    xq = unpack_weight(x_words, x_scales)[:, unstriped(offs)]
    y = mxq(f64(w1), 0, "e4m3").T @ xq
    c = 0.5 * (np.tanh(mxq(f64(w2), 0, "e4m3").T @ xq))
    cp = relu(c)
    z = y - (cp * (y - (y[np.arange(H)[:, None], runs(west, H)]))) - ((c - cp) * (y[np.arange(H)[:, None], runs(east, H)] - y))
    return mxq(f64(w3), 0, "e4m3").T @ mxq(z, 0, "e4m3")

@@ -1,0 +1,237 @@
+from contextlib import ExitStack
+
+import concourse.mybir as mybir
+from concourse.masks import make_identity
+
+K, T, S, N, H = 1024, 2048, 512, 512, 512
+FLOPS = 2 * (2 * K * H * S + H * N * S)
+
+F32 = mybir.dt.float32
+BF16 = mybir.dt.bfloat16
+I32 = mybir.dt.int32
+U32 = mybir.dt.uint32
+U16 = mybir.dt.uint16
+U8 = mybir.dt.uint8
+FP8X4 = mybir.dt.float8_e4m3fn_x4
+ALU = mybir.AluOpType
+ACT = mybir.ActivationFunctionType
+
+P = 128
+PACK = 4
+K_PASS = P * PACK
+PASSES = K // K_PASS
+TILES = H // P
+BLOCKS = S // P
+CHUNKS = ((0, 256), (256, 128), (384, 128))
+
+
+def tile_picked_advect_none_p_kernel(
+    tc, x_words, x_scales, w1, w2, w3, offs, east, west, out
+):
+    nc = tc.nc
+    with ExitStack() as ctx:
+        sb = ctx.enter_context(tc.tile_pool(name="sb", bufs=1))
+        psum = ctx.enter_context(tc.psum_pool(name="psum", bufs=1))
+
+        def tile(shape, dtype, name):
+            return sb.tile(shape, dtype, name=name, align_bytes=64)
+
+        def bank(index, shape):
+            return psum.tile(shape, F32, name="bank%d" % index)
+
+        offs_sb = sb.tile([P, S // 16], U16, name="offs_sb")
+        west_sb = sb.tile([P, S // 16], U16, name="west_sb")
+        east_sb = sb.tile([P, S // 16], U16, name="east_sb")
+        scale_table = tile([P, T], U8, "scale_table")
+        nc.vector.memset(scale_table[:].bitcast(I32), 0)
+        warm = tile([P, 1], F32, "warm")
+        nc.vector.memset(warm[:], 0.0)
+        warm_out = tile([P, 1], F32, "warm_out")
+        nc.scalar.activation(out=warm_out[:], in_=warm[:], func=ACT.Tanh)
+        ident = tile([P, P], F32, "ident")
+        make_identity(nc, ident[:])
+
+        word_table = [tile([P, T], I32, "word_table%d" % z) for z in range(PASSES)]
+
+        def load_words(z):
+            nc.sync.dma_start(
+                out=word_table[z][:], in_=x_words[z].rearrange("p c r -> p (c r)").bitcast(I32)
+            )
+
+        def load_rows(w, z, name):
+            raw = tile([P, PACK, H], F32, name)
+            nc.sync.dma_start(
+                out=raw[:], in_=w[z * K_PASS : (z + 1) * K_PASS, :].rearrange("(p j) c -> p j c", j=PACK)
+            )
+            return raw
+
+        nc.sync.dma_start(offs_sb[:], offs)
+        load_words(0)
+        for q in range(4):
+            nc.scalar.dma_start(
+                out=scale_table[32 * q : 32 * q + 4 * PASSES, :].bitcast(I32),
+                in_=x_scales[:, 4 * q : 4 * q + 4, :].bitcast(I32),
+            )
+        w1_raw = [load_rows(w1, 0, "w1_raw0")]
+        load_words(1)
+        w1_raw.append(load_rows(w1, 1, "w1_raw1"))
+        nc.sync.dma_start(west_sb[:], west)
+        nc.sync.dma_start(east_sb[:], east)
+        w2_raw = [load_rows(w2, z, "w2_raw%d" % z) for z in range(PASSES)]
+        w3_raw = load_rows(w3, 0, "w3_raw")
+
+        def copy_on(engine, dst, src):
+            if engine == "vector":
+                nc.vector.tensor_copy(out=dst, in_=src)
+            else:
+                nc.scalar.copy(out=dst, in_=src)
+
+        def cast(engine, raw, t, grouped):
+            copy_on(
+                engine,
+                grouped.rearrange("p (g q i j) -> p g q j i", g=8, q=4, i=4),
+                raw[:].rearrange("p j (g t q i) -> p t g q j i", g=8, t=TILES, q=4)[:, t],
+            )
+
+        def quantize(grouped, name):
+            width = grouped.shape[1] // PACK
+            codes = tile([P, width], U32, name + "_codes")
+            scales = tile([P, width], U8, name + "_scales")
+            nc.vector.quantize_mx(out=codes[:].bitcast(FP8X4), scales=scales[:], in_=grouped[:])
+            return codes, scales
+
+        def quantize_by_tile(engines, raw, name):
+            grouped = [tile([P, K_PASS], BF16, "%s_g%d" % (name, t)) for t in range(TILES)]
+            for t in range(TILES):
+                cast(engines[t], raw, t, grouped[t][:])
+            pairs = [quantize(grouped[t], "%s_%d" % (name, t)) for t in range(TILES)]
+            return [(codes[:], scales[:]) for codes, scales in pairs]
+
+        def quantize_whole(engine, raw, name):
+            grouped = tile([P, TILES * K_PASS], BF16, name + "_g")
+            for t in range(TILES):
+                cast(engine, raw, t, grouped[:, t * K_PASS : (t + 1) * K_PASS])
+            codes, scales = quantize(grouped, name)
+            return [(codes[:, t * P : (t + 1) * P], scales[:, t * P : (t + 1) * P]) for t in range(TILES)]
+
+        x_codes = [tile([P, S], U32, "x_codes%d" % z) for z in range(PASSES)]
+        x_scale = tile([P, S], U8, "x_scale")
+
+        def gather_words(z):
+            nc.vector.tensor_copy(out=x_codes[z][:], in_=word_table[z][:].bitcast(U32).indirect(offs_sb[:]))
+
+        def product(acc, wq, z):
+            codes, scales = wq
+            nc.tensor.matmul_mx(
+                out=acc[:],
+                lhsT=codes.bitcast(FP8X4),
+                lhsT_scale=scales,
+                rhs=x_codes[z][:].bitcast(FP8X4),
+                rhs_scale=x_scale[4 * z : P, :],
+                start=(z == 0),
+                stop=(z == PASSES - 1),
+            )
+
+        gather_words(0)
+        nc.vector.tensor_copy(out=x_scale[:], in_=scale_table[:].indirect(offs_sb[:]))
+        y_acc = [bank(t, [P, S]) for t in range(TILES)]
+        w1q = quantize_whole("vector", w1_raw[0], "w1p0")
+        for t in range(TILES):
+            product(y_acc[t], w1q[t], 0)
+        gather_words(1)
+        w1q = quantize_by_tile(("vector", "vector", "scalar", "scalar"), w1_raw[1], "w1p1")
+        half = [tile([P, S], F32, "half%d" % t) for t in range(TILES)]
+        minus_half = [tile([P, S], F32, "minus_half%d" % t) for t in range(TILES)]
+        for t in range(TILES):
+            product(y_acc[t], w1q[t], 1)
+            nc.scalar.activation(out=half[t][:], in_=y_acc[t][:], func=ACT.Copy, scale=0.5)
+            nc.scalar.activation(out=minus_half[t][:], in_=y_acc[t][:], func=ACT.Copy, scale=-0.5)
+
+        zt_acc = [bank(TILES + b, [P, H]) for b in range(BLOCKS)]
+
+        def add_turned(b, t, src, start=False, stop=False):
+            nc.tensor.matmul(
+                zt_acc[b][:, t * P : (t + 1) * P], src, ident[:], start=start, stop=stop, is_transpose=True
+            )
+
+        def differences(n, c0, width, t):
+            cols = slice(c0, c0 + width)
+            lists = slice(c0 // 16, (c0 + width) // 16)
+            d_west = tile([P, width], F32, "d_west%d_%d" % (n % 2, t))
+            d_east = tile([P, width], F32, "d_east%d_%d" % (n % 2, t))
+            nc.vector.tensor_tensor(d_west[:], half[t][:].indirect(west_sb[:, lists]), minus_half[t][:, cols], ALU.add)
+            nc.vector.tensor_tensor(d_east[:], minus_half[t][:].indirect(east_sb[:, lists]), half[t][:, cols], ALU.add)
+            return d_west, d_east
+
+        c_acc = [bank(t, [P, S]) for t in range(TILES)]
+        w2q = quantize_whole("vector", w2_raw[0], "w2p0")
+        for t in range(TILES):
+            product(c_acc[t], w2q[t], 0)
+        w2q = quantize_by_tile(("scalar",) * TILES, w2_raw[1], "w2p1")
+        th = [tile([P, S], F32, "th%d" % t) for t in range(TILES)]
+        for t in range(TILES):
+            product(c_acc[t], w2q[t], 1)
+            nc.scalar.activation(out=th[t][:], in_=c_acc[t][:], func=ACT.Tanh)
+
+        for t in range(TILES):
+            for b in range(BLOCKS):
+                add_turned(b, t, half[t][:, b * P : (b + 1) * P], start=(t == 0))
+                add_turned(b, t, half[t][:, b * P : (b + 1) * P])
+
+        w3_grouped = tile([P, N * PACK], BF16, "w3_grouped")
+        nc.scalar.copy(
+            out=w3_grouped[:].rearrange("p (c i j) -> p c j i", i=4, j=PACK),
+            in_=w3_raw[:].rearrange("p j (c i) -> p c j i", i=4),
+        )
+        w3_codes, w3_scales = quantize(w3_grouped, "w3")
+
+        out_view = out.rearrange("(mt p) c -> p mt c", p=P)
+        back_bank = (0, 3, 5)
+        out_banks = ((1, 2), (4, 0), (3, 1))
+        for n, (c0, width) in enumerate(CHUNKS):
+            cols = slice(c0, c0 + width)
+            blocks = range(c0 // P, (c0 + width) // P)
+            diffs = [differences(n, c0, width, t) for t in range(TILES)]
+            for t in range(TILES):
+                d_west, d_east = diffs[t]
+                from_west = tile([P, width], F32, "from_west%d_%d" % (c0, t))
+                from_east = tile([P, width], F32, "from_east%d_%d" % (c0, t))
+                nc.vector.scalar_tensor_tensor(from_west[:], th[t][:, cols], 0.0, d_west[:], ALU.max, ALU.mult)
+                nc.vector.scalar_tensor_tensor(from_east[:], th[t][:, cols], 0.0, d_east[:], ALU.min, ALU.mult)
+                for b in blocks:
+                    local = slice(b * P - c0, (b + 1) * P - c0)
+                    add_turned(b, t, from_west[:, local])
+                    add_turned(b, t, from_east[:, local], stop=(t == TILES - 1))
+            back = bank(back_bank[n], [P, len(blocks), 2, P])
+            for b in blocks:
+                zt = tile([P, H], BF16, "zt%d" % b)
+                nc.scalar.copy(
+                    out=zt[:].rearrange("c (g t r) -> c g t r", g=8, t=TILES),
+                    in_=zt_acc[b][:].rearrange("c (t g r) -> c g t r", g=8, t=TILES),
+                )
+                words = zt[:].bitcast(F32)
+                for u in range(2):
+                    nc.tensor.transpose(back[:, b - blocks[0], u, :], words[:, u : H // 2 : 2], ident[:])
+            z_grouped = tile([P, width * PACK], BF16, "z_grouped%d" % n)
+            nc.scalar.copy(
+                out=z_grouped[:].bitcast(F32).rearrange("p (b r u) -> p b r u", u=2, r=P),
+                in_=back[:].rearrange("p b u r -> p b r u"),
+            )
+            z_codes, z_scales = quantize(z_grouped, "z%d" % n)
+            for h in range(2):
+                acc = bank(out_banks[n][h], [P, 2, width])
+                for m in range(2):
+                    mt = 2 * h + m
+                    nc.tensor.matmul_mx(
+                        out=acc[:, m, :],
+                        lhsT=w3_codes[:, mt * P : (mt + 1) * P].bitcast(FP8X4),
+                        lhsT_scale=w3_scales[:, mt * P : (mt + 1) * P],
+                        rhs=z_codes[:].bitcast(FP8X4),
+                        rhs_scale=z_scales[:],
+                        start=True,
+                        stop=True,
+                    )
+                result = tile([P, 2, width], F32, "result%d_%d" % (n, h))
+                last = n == len(CHUNKS) - 1
+                copy_on("vector" if last and h == 1 else "scalar", result[:], acc[:])
+                nc.sync.dma_start(out=out_view[:, 2 * h : 2 * h + 2, cols], in_=result[:])

@@ -22,6 +22,7 @@ K_PASS = P * PACK
 PASSES = K // K_PASS
 TILES = H // P
 BLOCKS = S // P
+HALF = S // 2
 CHUNKS = ((0, 256), (256, 128), (384, 128))
 
 
@@ -65,13 +66,19 @@ def tile_picked_advect_none_p_kernel(
             )
             return raw
 
-        nc.sync.dma_start(offs_sb[:], offs)
+        scale_rows = tile([P, T // 4], I32, "scale_rows")
+
+        def load_scales(z):
+            for q in range(4):
+                nc.sync.dma_start(
+                    out=scale_rows[32 * q + 4 * z : 32 * q + 4 * z + 4, :],
+                    in_=x_scales[z, 4 * q : 4 * q + 4, :].bitcast(I32),
+                )
+
+        load_scales(0)
         load_words(0)
-        for q in range(4):
-            nc.scalar.dma_start(
-                out=scale_table[32 * q : 32 * q + 4 * PASSES, :].bitcast(I32),
-                in_=x_scales[:, 4 * q : 4 * q + 4, :].bitcast(I32),
-            )
+        nc.sync.dma_start(offs_sb[:], offs)
+        load_scales(1)
         w1_raw = [load_rows(w1, 0, "w1_raw0")]
         load_words(1)
         w1_raw.append(load_rows(w1, 1, "w1_raw1"))
@@ -97,18 +104,19 @@ def tile_picked_advect_none_p_kernel(
             width = grouped.shape[1] // PACK
             codes = tile([P, width], U32, name + "_codes")
             scales = tile([P, width], U8, name + "_scales")
-            nc.vector.quantize_mx(out=codes[:].bitcast(FP8X4), scales=scales[:], in_=grouped[:])
+            nc.vector.quantize_mx(out=codes[:].bitcast(FP8X4), scales=scales[:], in_=grouped)
             return codes, scales
 
         def quantize_by_tile(engines, raw, name):
             grouped = [tile([P, K_PASS], BF16, "%s_g%d" % (name, t)) for t in range(TILES)]
             for t in range(TILES):
                 cast(engines[t], raw, t, grouped[t][:])
-            pairs = [quantize(grouped[t], "%s_%d" % (name, t)) for t in range(TILES)]
+            pairs = [quantize(grouped[t][:], "%s_%d" % (name, t)) for t in range(TILES)]
             return [(codes[:], scales[:]) for codes, scales in pairs]
 
-        def quantize_whole(engine, raw, name):
-            grouped = tile([P, TILES * K_PASS], BF16, name + "_g")
+        def quantize_whole(engine, raw, name, grouped=None):
+            if grouped is None:
+                grouped = tile([P, TILES * K_PASS], BF16, name + "_g")[:]
             for t in range(TILES):
                 cast(engine, raw, t, grouped[:, t * K_PASS : (t + 1) * K_PASS])
             codes, scales = quantize(grouped, name)
@@ -133,9 +141,12 @@ def tile_picked_advect_none_p_kernel(
             )
 
         gather_words(0)
+        for q in range(4):
+            live = slice(32 * q, 32 * q + 4 * PASSES)
+            nc.vector.tensor_copy(out=scale_table[live, :].bitcast(I32), in_=scale_rows[live, :])
         nc.vector.tensor_copy(out=x_scale[:], in_=scale_table[:].indirect(offs_sb[:]))
         y_acc = [bank(t, [P, S]) for t in range(TILES)]
-        w1q = quantize_whole("vector", w1_raw[0], "w1p0")
+        w1q = quantize_by_tile(("scalar", "scalar", "vector", "vector"), w1_raw[0], "w1p0")
         for t in range(TILES):
             product(y_acc[t], w1q[t], 0)
         gather_words(1)
@@ -154,24 +165,29 @@ def tile_picked_advect_none_p_kernel(
                 zt_acc[b][:, t * P : (t + 1) * P], src, ident[:], start=start, stop=stop, is_transpose=True
             )
 
-        def differences(n, c0, width, t):
+        d_wide = tile([P, TILES * 2 * HALF], F32, "d_wide")
+        d_narrow = tile([P, TILES * 2 * P], F32, "d_narrow")
+        last_terms = tile([P, TILES * 2 * P], F32, "last_terms")
+
+        def differences(c0, width):
             cols = slice(c0, c0 + width)
             lists = slice(c0 // 16, (c0 + width) // 16)
-            d_west = tile([P, width], F32, "d_west%d_%d" % (n % 2, t))
-            d_east = tile([P, width], F32, "d_east%d_%d" % (n % 2, t))
-            nc.vector.tensor_tensor(d_west[:], half[t][:].indirect(west_sb[:, lists]), minus_half[t][:, cols], ALU.add)
-            nc.vector.tensor_tensor(d_east[:], minus_half[t][:].indirect(east_sb[:, lists]), half[t][:, cols], ALU.add)
+            d_view = (d_wide if width == HALF else d_narrow)[:].rearrange("p (t s c) -> p s t c", t=TILES, s=2)
+            d_west, d_east = d_view[:, 0], d_view[:, 1]
+            for t in range(TILES):
+                nc.vector.tensor_tensor(d_west[:, t, :], half[t][:].indirect(west_sb[:, lists]), minus_half[t][:, cols], ALU.add)
+                nc.vector.tensor_tensor(d_east[:, t, :], minus_half[t][:].indirect(east_sb[:, lists]), half[t][:, cols], ALU.add)
             return d_west, d_east
 
         c_acc = [bank(t, [P, S]) for t in range(TILES)]
         w2q = quantize_whole("vector", w2_raw[0], "w2p0")
         for t in range(TILES):
             product(c_acc[t], w2q[t], 0)
-        w2q = quantize_by_tile(("scalar",) * TILES, w2_raw[1], "w2p1")
-        th = [tile([P, S], F32, "th%d" % t) for t in range(TILES)]
+        w2q = quantize_whole("scalar", w2_raw[1], "w2p1", d_narrow[:].bitcast(BF16))
+        th = tile([P, TILES, S], F32, "th")
         for t in range(TILES):
             product(c_acc[t], w2q[t], 1)
-            nc.scalar.activation(out=th[t][:], in_=c_acc[t][:], func=ACT.Tanh)
+            nc.scalar.activation(out=th[:, t, :], in_=c_acc[t][:], func=ACT.Tanh)
 
         for t in range(TILES):
             for b in range(BLOCKS):
@@ -183,7 +199,7 @@ def tile_picked_advect_none_p_kernel(
             out=w3_grouped[:].rearrange("p (c i j) -> p c j i", i=4, j=PACK),
             in_=w3_raw[:].rearrange("p j (c i) -> p c j i", i=4),
         )
-        w3_codes, w3_scales = quantize(w3_grouped, "w3")
+        w3_codes, w3_scales = quantize(w3_grouped[:], "w3")
 
         out_view = out.rearrange("(mt p) c -> p mt c", p=P)
         back_bank = (0, 3, 5)
@@ -191,31 +207,42 @@ def tile_picked_advect_none_p_kernel(
         for n, (c0, width) in enumerate(CHUNKS):
             cols = slice(c0, c0 + width)
             blocks = range(c0 // P, (c0 + width) // P)
-            diffs = [differences(n, c0, width, t) for t in range(TILES)]
-            for t in range(TILES):
-                d_west, d_east = diffs[t]
-                from_west = tile([P, width], F32, "from_west%d_%d" % (c0, t))
-                from_east = tile([P, width], F32, "from_east%d_%d" % (c0, t))
-                nc.vector.scalar_tensor_tensor(from_west[:], th[t][:, cols], 0.0, d_west[:], ALU.max, ALU.mult)
-                nc.vector.scalar_tensor_tensor(from_east[:], th[t][:, cols], 0.0, d_east[:], ALU.min, ALU.mult)
-                for b in blocks:
-                    local = slice(b * P - c0, (b + 1) * P - c0)
-                    add_turned(b, t, from_west[:, local])
-                    add_turned(b, t, from_east[:, local], stop=(t == TILES - 1))
+            d_west, d_east = differences(c0, width)
+            if n == 2:
+                terms = last_terms
+            else:
+                terms = tile([P, TILES * 2 * width], F32, "terms%d" % n)
+            view = terms[:].rearrange("p (t s c) -> p s t c", t=TILES, s=2)
+            from_west, from_east = view[:, 0], view[:, 1]
+            nc.vector.scalar_tensor_tensor(from_west, th[:, :, cols], 0.0, d_west, ALU.max, ALU.mult)
+            for b in blocks:
+                for t in range(TILES):
+                    add_turned(b, t, from_west[:, t, b * P - c0 : (b + 1) * P - c0])
+            for ts in ((slice(0, 3), slice(3, 4)) if n == len(CHUNKS) - 1 else (slice(0, 4),)):
+                nc.vector.scalar_tensor_tensor(from_east[:, ts, :], th[:, ts, cols], 0.0, d_east[:, ts, :], ALU.min, ALU.mult)
+            for b in blocks:
+                for t in range(TILES):
+                    add_turned(b, t, from_east[:, t, b * P - c0 : (b + 1) * P - c0], stop=(t == TILES - 1))
             back = bank(back_bank[n], [P, len(blocks), 2, P])
             for b in blocks:
                 zt = tile([P, H], BF16, "zt%d" % b)
-                nc.scalar.copy(
-                    out=zt[:].rearrange("c (g t r) -> c g t r", g=8, t=TILES),
-                    in_=zt_acc[b][:].rearrange("c (t g r) -> c g t r", g=8, t=TILES),
+                copy_on(
+                    "vector" if b == BLOCKS - 1 else "scalar",
+                    zt[:].rearrange("c (g t r) -> c g t r", g=8, t=TILES),
+                    zt_acc[b][:].rearrange("c (t g r) -> c g t r", g=8, t=TILES),
                 )
                 words = zt[:].bitcast(F32)
                 for u in range(2):
                     nc.tensor.transpose(back[:, b - blocks[0], u, :], words[:, u : H // 2 : 2], ident[:])
-            z_grouped = tile([P, width * PACK], BF16, "z_grouped%d" % n)
-            nc.scalar.copy(
-                out=z_grouped[:].bitcast(F32).rearrange("p (b r u) -> p b r u", u=2, r=P),
-                in_=back[:].rearrange("p b u r -> p b r u"),
+            if n == 0:
+                z_words = last_terms[:, 4 * P :]
+            else:
+                z_words = tile([P, width * 2], F32, "z_words%d" % n)[:]
+            z_grouped = z_words.bitcast(BF16)
+            copy_on(
+                "vector" if n == 2 else "scalar",
+                z_words.rearrange("p (b r u) -> p b r u", u=2, r=P),
+                back[:].rearrange("p b u r -> p b r u"),
             )
             z_codes, z_scales = quantize(z_grouped, "z%d" % n)
             for h in range(2):
@@ -232,6 +259,6 @@ def tile_picked_advect_none_p_kernel(
                         stop=True,
                     )
                 result = tile([P, 2, width], F32, "result%d_%d" % (n, h))
-                last = n == len(CHUNKS) - 1
-                copy_on("vector" if last and h == 1 else "scalar", result[:], acc[:])
-                nc.sync.dma_start(out=out_view[:, 2 * h : 2 * h + 2, cols], in_=result[:])
+                copy_on("vector" if n == 2 and h == 1 else "scalar", result[:], acc[:])
+                queue = nc.scalar if n == 2 and h == 0 else nc.sync
+                queue.dma_start(out=out_view[:, 2 * h : 2 * h + 2, cols], in_=result[:])

@@ -167,7 +167,7 @@ def tile_picked_advect_none_p_kernel(
 
         d_wide = tile([P, TILES * 2 * HALF], F32, "d_wide")
         d_narrow = tile([P, TILES * 2 * P], F32, "d_narrow")
-        last_terms = tile([P, TILES * 2 * P], F32, "last_terms")
+        last_terms = [tile([P, 2 * HALF], F32, "last_terms%d" % t) for t in range(TILES)]
 
         def differences(c0, width):
             cols = slice(c0, c0 + width)
@@ -194,35 +194,76 @@ def tile_picked_advect_none_p_kernel(
                 add_turned(b, t, half[t][:, b * P : (b + 1) * P], start=(t == 0))
                 add_turned(b, t, half[t][:, b * P : (b + 1) * P])
 
-        w3_grouped = tile([P, N * PACK], BF16, "w3_grouped")
-        nc.scalar.copy(
-            out=w3_grouped[:].rearrange("p (c i j) -> p c j i", i=4, j=PACK),
-            in_=w3_raw[:].rearrange("p j (c i) -> p c j i", i=4),
-        )
-        w3_codes, w3_scales = quantize(w3_grouped[:], "w3")
+        last_cols = slice(S - P, S)
+        gates = tile([P, 3, TILES, P], F32, "gates")
+        nc.scalar.activation(out=gates[:, 0], in_=th[:, :, last_cols], func=ACT.Relu)
+        nc.scalar.activation(out=gates[:, 1], in_=th[:, :, last_cols], func=ACT.Relu, scale=-1.0)
+        nc.scalar.activation(out=gates[:, 2], in_=th[:, :, last_cols], func=ACT.Abs)
 
         out_view = out.rearrange("(mt p) c -> p mt c", p=P)
         back_bank = (0, 3, 5)
-        out_banks = ((1, 2), (4, 0), (3, 1))
+        out_banks = ((1, 2), (4, 0), (3, 1, 2, 6))
+
+        def quantize_w3():
+            grouped = tile([P, N * PACK], BF16, "w3_grouped")
+            for mt in range(TILES):
+                nc.scalar.copy(
+                    out=grouped[:, mt * K_PASS : (mt + 1) * K_PASS].rearrange("p (c i j) -> p c j i", i=4, j=PACK),
+                    in_=w3_raw[:, :, mt * P : (mt + 1) * P].rearrange("p j (c i) -> p c j i", i=4),
+                )
+            return quantize(grouped[:], "w3")
+
+        def finish(n, w3q, zq):
+            (w3_codes, w3_scales), (z_codes, z_scales) = w3q, zq
+            c0, width = CHUNKS[n]
+            cols = slice(c0, c0 + width)
+            rows = TILES // len(out_banks[n])
+            for h, index in enumerate(out_banks[n]):
+                acc = bank(index, [P, rows, width])
+                for m in range(rows):
+                    mt = rows * h + m
+                    nc.tensor.matmul_mx(
+                        out=acc[:, m, :],
+                        lhsT=w3_codes[:, mt * P : (mt + 1) * P].bitcast(FP8X4),
+                        lhsT_scale=w3_scales[:, mt * P : (mt + 1) * P],
+                        rhs=z_codes[:].bitcast(FP8X4),
+                        rhs_scale=z_scales[:],
+                        start=True,
+                        stop=True,
+                    )
+                result = tile([P, rows, width], F32, "result%d_%d" % (n, h))
+                copy_on("vector" if n == 2 and h % 2 == 1 else "scalar", result[:], acc[:])
+                queue = nc.scalar if n == 2 and h == 2 else nc.sync
+                queue.dma_start(out=out_view[:, rows * h : rows * (h + 1), cols], in_=result[:])
+
+        quantized = []
         for n, (c0, width) in enumerate(CHUNKS):
             cols = slice(c0, c0 + width)
             blocks = range(c0 // P, (c0 + width) // P)
-            d_west, d_east = differences(c0, width)
-            if n == 2:
-                terms = last_terms
-            else:
+            if n < 2:
+                d_west, d_east = differences(c0, width)
                 terms = tile([P, TILES * 2 * width], F32, "terms%d" % n)
-            view = terms[:].rearrange("p (t s c) -> p s t c", t=TILES, s=2)
-            from_west, from_east = view[:, 0], view[:, 1]
-            nc.vector.scalar_tensor_tensor(from_west, th[:, :, cols], 0.0, d_west, ALU.max, ALU.mult)
-            for b in blocks:
+                view = terms[:].rearrange("p (t s c) -> p s t c", t=TILES, s=2)
+                for side, (op, d) in enumerate(((ALU.max, d_west), (ALU.min, d_east))):
+                    nc.vector.scalar_tensor_tensor(view[:, side], th[:, :, cols], 0.0, d, op, ALU.mult)
+                    for b in blocks:
+                        for t in range(TILES):
+                            add_turned(
+                                b, t, view[:, side, t, b * P - c0 : (b + 1) * P - c0],
+                                stop=(side == 1 and t == TILES - 1),
+                            )
+            else:
+                lists = slice(c0 // 16, (c0 + width) // 16)
+                leaving = tile([P, TILES, P], F32, "leaving")
                 for t in range(TILES):
-                    add_turned(b, t, from_west[:, t, b * P - c0 : (b + 1) * P - c0])
-            for ts in ((slice(0, 3), slice(3, 4)) if n == len(CHUNKS) - 1 else (slice(0, 4),)):
-                nc.vector.scalar_tensor_tensor(from_east[:, ts, :], th[:, ts, cols], 0.0, d_east[:, ts, :], ALU.min, ALU.mult)
-            for b in blocks:
+                    nc.vector.tensor_tensor(leaving[:, t, :], gates[:, 2, t, :], minus_half[t][:, cols], ALU.mult)
+                    add_turned(blocks[0], t, leaving[:, t, :])
                 for t in range(TILES):
-                    add_turned(b, t, from_east[:, t, b * P - c0 : (b + 1) * P - c0], stop=(t == TILES - 1))
+                    for side, neighbours in enumerate((west_sb, east_sb)):
+                        term = last_terms[t][:, side * P : (side + 1) * P]
+                        nc.vector.tensor_tensor(term, half[t][:].indirect(neighbours[:, lists]), gates[:, side, t, :], ALU.mult)
+                        add_turned(blocks[0], t, term, stop=(side == 1 and t == TILES - 1))
+                finish(1, w3q, quantized[1])
             back = bank(back_bank[n], [P, len(blocks), 2, P])
             for b in blocks:
                 zt = tile([P, H], BF16, "zt%d" % b)
@@ -235,30 +276,16 @@ def tile_picked_advect_none_p_kernel(
                 for u in range(2):
                     nc.tensor.transpose(back[:, b - blocks[0], u, :], words[:, u : H // 2 : 2], ident[:])
             if n == 0:
-                z_words = last_terms[:, 4 * P :]
+                z_words = last_terms[TILES - 1][:]
             else:
                 z_words = tile([P, width * 2], F32, "z_words%d" % n)[:]
             z_grouped = z_words.bitcast(BF16)
-            copy_on(
-                "vector" if n == 2 else "scalar",
-                z_words.rearrange("p (b r u) -> p b r u", u=2, r=P),
-                back[:].rearrange("p b u r -> p b r u"),
+            nc.scalar.copy(
+                out=z_words.rearrange("p (b r u) -> p b r u", u=2, r=P),
+                in_=back[:].rearrange("p b u r -> p b r u"),
             )
-            z_codes, z_scales = quantize(z_grouped, "z%d" % n)
-            for h in range(2):
-                acc = bank(out_banks[n][h], [P, 2, width])
-                for m in range(2):
-                    mt = 2 * h + m
-                    nc.tensor.matmul_mx(
-                        out=acc[:, m, :],
-                        lhsT=w3_codes[:, mt * P : (mt + 1) * P].bitcast(FP8X4),
-                        lhsT_scale=w3_scales[:, mt * P : (mt + 1) * P],
-                        rhs=z_codes[:].bitcast(FP8X4),
-                        rhs_scale=z_scales[:],
-                        start=True,
-                        stop=True,
-                    )
-                result = tile([P, 2, width], F32, "result%d_%d" % (n, h))
-                copy_on("vector" if n == 2 and h == 1 else "scalar", result[:], acc[:])
-                queue = nc.scalar if n == 2 and h == 0 else nc.sync
-                queue.dma_start(out=out_view[:, 2 * h : 2 * h + 2, cols], in_=result[:])
+            quantized.append(quantize(z_grouped, "z%d" % n))
+            if n == 1:
+                w3q = quantize_w3()
+                finish(0, w3q, quantized[0])
+        finish(2, w3q, quantized[2])

@@ -1,7 +1,6 @@
 from contextlib import ExitStack
 
 import concourse.mybir as mybir
-from concourse.masks import make_identity
 
 K, T, S, N, H = 1024, 2048, 512, 512, 512
 FLOPS = 2 * (2 * K * H * S + H * N * S)
@@ -21,9 +20,9 @@ PACK = 4
 K_PASS = P * PACK
 PASSES = K // K_PASS
 TILES = H // P
-BLOCKS = S // P
-HALF = S // 2
-CHUNKS = ((0, 256), (256, 128), (384, 128))
+FUSED = 2
+CHUNKS = ((0, 128), (128, 128), (256, 128), (384, 128))
+EAST_CHUNKS = ((0, 128), (128, 256), (384, 128))
 
 
 def tile_picked_advect_none_p_kernel(
@@ -44,13 +43,7 @@ def tile_picked_advect_none_p_kernel(
         west_sb = sb.tile([P, S // 16], U16, name="west_sb")
         east_sb = sb.tile([P, S // 16], U16, name="east_sb")
         scale_table = tile([P, T], U8, "scale_table")
-        nc.vector.memset(scale_table[:].bitcast(I32), 0)
-        warm = tile([P, 1], F32, "warm")
-        nc.vector.memset(warm[:], 0.0)
-        warm_out = tile([P, 1], F32, "warm_out")
-        nc.scalar.activation(out=warm_out[:], in_=warm[:], func=ACT.Tanh)
-        ident = tile([P, P], F32, "ident")
-        make_identity(nc, ident[:])
+        nc.gpsimd.memset(scale_table[:].bitcast(I32), 0)
 
         word_table = [tile([P, T], I32, "word_table%d" % z) for z in range(PASSES)]
 
@@ -66,26 +59,27 @@ def tile_picked_advect_none_p_kernel(
             )
             return raw
 
-        scale_rows = tile([P, T // 4], I32, "scale_rows")
+        def load_halves(w, z, name):
+            rows = w[z * K_PASS : (z + 1) * K_PASS, :].rearrange("(p j) c -> p j c", j=PACK)
+            parts = [tile([P, PACK, H // 2], F32, "%s_%d" % (name, h)) for h in range(2)]
+            for h in range(2):
+                nc.sync.dma_start(out=parts[h][:], in_=rows[:, :, h * H // 2 : (h + 1) * H // 2])
+            return parts
 
-        def load_scales(z):
-            for q in range(4):
-                nc.sync.dma_start(
-                    out=scale_rows[32 * q + 4 * z : 32 * q + 4 * z + 4, :],
-                    in_=x_scales[z, 4 * q : 4 * q + 4, :].bitcast(I32),
-                )
-
-        load_scales(0)
         load_words(0)
         nc.sync.dma_start(offs_sb[:], offs)
-        load_scales(1)
-        w1_raw = [load_rows(w1, 0, "w1_raw0")]
+        for q in range(4):
+            nc.sync.dma_start(
+                out=scale_table[32 * q : 32 * q + 4 * PASSES, :].bitcast(I32),
+                in_=x_scales[:, 4 * q : 4 * q + 4, :].bitcast(I32),
+            )
+        w2_raw = [load_rows(w2, 0, "w2_raw0")]
         load_words(1)
-        w1_raw.append(load_rows(w1, 1, "w1_raw1"))
-        nc.sync.dma_start(west_sb[:], west)
+        w2_raw.append(load_halves(w2, 1, "w2_raw1"))
+        w1_raw = [load_rows(w1, 0, "w1_raw0"), load_halves(w1, 1, "w1_raw1")]
+        w3_all = load_rows(w3, 0, "w3_all")
         nc.sync.dma_start(east_sb[:], east)
-        w2_raw = [load_rows(w2, z, "w2_raw%d" % z) for z in range(PASSES)]
-        w3_raw = load_rows(w3, 0, "w3_raw")
+        nc.sync.dma_start(west_sb[:], west)
 
         def copy_on(engine, dst, src):
             if engine == "vector":
@@ -93,11 +87,11 @@ def tile_picked_advect_none_p_kernel(
             else:
                 nc.scalar.copy(out=dst, in_=src)
 
-        def cast(engine, raw, t, grouped):
+        def cast(engine, grouped, first, raw):
             copy_on(
                 engine,
-                grouped.rearrange("p (g q i j) -> p g q j i", g=8, q=4, i=4),
-                raw[:].rearrange("p j (g t q i) -> p t g q j i", g=8, t=TILES, q=4)[:, t],
+                grouped[:, :, first : first + raw.shape[2]].rearrange("p t (m j) -> p m j t", j=PACK),
+                raw.rearrange("p j (m t) -> p m j t", t=TILES),
             )
 
         def quantize(grouped, name):
@@ -107,20 +101,19 @@ def tile_picked_advect_none_p_kernel(
             nc.vector.quantize_mx(out=codes[:].bitcast(FP8X4), scales=scales[:], in_=grouped)
             return codes, scales
 
-        def quantize_by_tile(engines, raw, name):
-            grouped = [tile([P, K_PASS], BF16, "%s_g%d" % (name, t)) for t in range(TILES)]
-            for t in range(TILES):
-                cast(engines[t], raw, t, grouped[t][:])
-            pairs = [quantize(grouped[t][:], "%s_%d" % (name, t)) for t in range(TILES)]
-            return [(codes[:], scales[:]) for codes, scales in pairs]
-
-        def quantize_whole(engine, raw, name, grouped=None):
-            if grouped is None:
-                grouped = tile([P, TILES * K_PASS], BF16, name + "_g")[:]
-            for t in range(TILES):
-                cast(engine, raw, t, grouped[:, t * K_PASS : (t + 1) * K_PASS])
-            codes, scales = quantize(grouped, name)
-            return [(codes[:, t * P : (t + 1) * P], scales[:, t * P : (t + 1) * P]) for t in range(TILES)]
+        def quantize_pass(shares, name, tiles_a_call):
+            grouped = tile([P, TILES, K_PASS], BF16, name + "_g")
+            first = 0
+            for engine, raw in shares:
+                cast(engine, grouped, first, raw)
+                first = first + raw.shape[2]
+            pairs = []
+            for t in range(0, TILES, tiles_a_call):
+                rows = grouped[:, t : t + tiles_a_call, :].rearrange("p t c -> p (t c)")
+                codes, scales = quantize(rows, "%s_%d" % (name, t))
+                for u in range(tiles_a_call):
+                    pairs.append((codes[:, u * P : (u + 1) * P], scales[:, u * P : (u + 1) * P]))
+            return pairs
 
         x_codes = [tile([P, S], U32, "x_codes%d" % z) for z in range(PASSES)]
         x_scale = tile([P, S], U8, "x_scale")
@@ -128,90 +121,76 @@ def tile_picked_advect_none_p_kernel(
         def gather_words(z):
             nc.vector.tensor_copy(out=x_codes[z][:], in_=word_table[z][:].bitcast(U32).indirect(offs_sb[:]))
 
-        def product(acc, wq, z):
+        def product(acc, wq, z, cells=slice(0, S)):
             codes, scales = wq
             nc.tensor.matmul_mx(
                 out=acc[:],
                 lhsT=codes.bitcast(FP8X4),
                 lhsT_scale=scales,
-                rhs=x_codes[z][:].bitcast(FP8X4),
-                rhs_scale=x_scale[4 * z : P, :],
+                rhs=x_codes[z][:, cells].bitcast(FP8X4),
+                rhs_scale=x_scale[4 * z : P, cells],
                 start=(z == 0),
                 stop=(z == PASSES - 1),
             )
 
         gather_words(0)
-        for q in range(4):
-            live = slice(32 * q, 32 * q + 4 * PASSES)
-            nc.vector.tensor_copy(out=scale_table[live, :].bitcast(I32), in_=scale_rows[live, :])
         nc.vector.tensor_copy(out=x_scale[:], in_=scale_table[:].indirect(offs_sb[:]))
-        y_acc = [bank(t, [P, S]) for t in range(TILES)]
-        w1q = quantize_by_tile(("scalar", "scalar", "vector", "vector"), w1_raw[0], "w1p0")
-        for t in range(TILES):
-            product(y_acc[t], w1q[t], 0)
-        gather_words(1)
-        w1q = quantize_by_tile(("vector", "vector", "scalar", "scalar"), w1_raw[1], "w1p1")
-        half = [tile([P, S], F32, "half%d" % t) for t in range(TILES)]
-        minus_half = [tile([P, S], F32, "minus_half%d" % t) for t in range(TILES)]
-        for t in range(TILES):
-            product(y_acc[t], w1q[t], 1)
-            nc.scalar.activation(out=half[t][:], in_=y_acc[t][:], func=ACT.Copy, scale=0.5)
-            nc.scalar.activation(out=minus_half[t][:], in_=y_acc[t][:], func=ACT.Copy, scale=-0.5)
-
-        zt_acc = [bank(TILES + b, [P, H]) for b in range(BLOCKS)]
-
-        def add_turned(b, t, src, start=False, stop=False):
-            nc.tensor.matmul(
-                zt_acc[b][:, t * P : (t + 1) * P], src, ident[:], start=start, stop=stop, is_transpose=True
-            )
-
-        d_wide = tile([P, TILES * 2 * HALF], F32, "d_wide")
-        d_narrow = tile([P, TILES * 2 * P], F32, "d_narrow")
-        last_terms = [tile([P, 2 * HALF], F32, "last_terms%d" % t) for t in range(TILES)]
-
-        def differences(c0, width):
-            cols = slice(c0, c0 + width)
-            lists = slice(c0 // 16, (c0 + width) // 16)
-            d_view = (d_wide if width == HALF else d_narrow)[:].rearrange("p (t s c) -> p s t c", t=TILES, s=2)
-            d_west, d_east = d_view[:, 0], d_view[:, 1]
-            for t in range(TILES):
-                nc.vector.tensor_tensor(d_west[:, t, :], half[t][:].indirect(west_sb[:, lists]), minus_half[t][:, cols], ALU.add)
-                nc.vector.tensor_tensor(d_east[:, t, :], minus_half[t][:].indirect(east_sb[:, lists]), half[t][:, cols], ALU.add)
-            return d_west, d_east
-
         c_acc = [bank(t, [P, S]) for t in range(TILES)]
-        w2q = quantize_whole("vector", w2_raw[0], "w2p0")
+        w2q = quantize_pass((("vector", w2_raw[0][:]),), "w2p0", 2)
         for t in range(TILES):
             product(c_acc[t], w2q[t], 0)
-        w2q = quantize_whole("scalar", w2_raw[1], "w2p1", d_narrow[:].bitcast(BF16))
+        gather_words(1)
+        w2q = quantize_pass(
+            (("scalar", w2_raw[1][0][:]), ("vector", w2_raw[1][1][:])),
+            "w2p1",
+            1,
+        )
         th = tile([P, TILES, S], F32, "th")
+        speed = tile([P, TILES, S], F32, "speed")
         for t in range(TILES):
             product(c_acc[t], w2q[t], 1)
             nc.scalar.activation(out=th[:, t, :], in_=c_acc[t][:], func=ACT.Tanh)
 
-        for t in range(TILES):
-            for b in range(BLOCKS):
-                add_turned(b, t, half[t][:, b * P : (b + 1) * P], start=(t == 0))
-                add_turned(b, t, half[t][:, b * P : (b + 1) * P])
+        nc.scalar.activation(out=speed[:, 0, :], in_=th[:, 0, :], func=ACT.Abs, scale=0.5)
 
-        last_cols = slice(S - P, S)
-        gates = tile([P, 3, TILES, P], F32, "gates")
-        nc.scalar.activation(out=gates[:, 0], in_=th[:, :, last_cols], func=ACT.Relu)
-        nc.scalar.activation(out=gates[:, 1], in_=th[:, :, last_cols], func=ACT.Relu, scale=-1.0)
-        nc.scalar.activation(out=gates[:, 2], in_=th[:, :, last_cols], func=ACT.Abs)
+        low, high = slice(0, S // 2), slice(S // 2, S)
+        y_parts = [(0, low, bank(TILES, [P, S // 2])), (0, high, bank(0, [P, S // 2]))]
+        y_parts.extend((t, slice(0, S), bank(TILES + t, [P, S])) for t in range(1, TILES))
+        w1q = quantize_pass((("vector", w1_raw[0][:]),), "w1p0", 4)
+        for t, cells, acc in y_parts:
+            product(acc, w1q[t], 0, cells)
+        w1q = quantize_pass((("vector", w1_raw[1][0][:]), ("vector", w1_raw[1][1][:])), "w1p1", 1)
+        forward = tile([P, FUSED, P], F32, "w1p1_g")
+        nc.vector.tensor_scalar_max(forward[:], th[:, 0:FUSED, 0:P], 0.0)
+        half = [tile([P, S], F32, "half%d" % t) for t in range(TILES)]
+        staying = tile([P, TILES, S], F32, "staying")
+
+        def copy_half(t, cells, acc):
+            nc.scalar.activation(out=half[t][:, cells], in_=acc[:], func=ACT.Copy, scale=0.5)
+
+        def stay(t, cells, acc):
+            nc.vector.scalar_tensor_tensor(staying[:, t, cells], speed[:, t, cells], 1.0, acc[:], ALU.subtract, ALU.mult)
+
+        for t, cells, acc in y_parts:
+            product(acc, w1q[t], 1, cells)
+        stay(*y_parts[1])
+        for part in y_parts:
+            copy_half(*part)
+        stay(*y_parts[0])
+        for part in y_parts[2:]:
+            nc.scalar.activation(out=speed[:, part[0], :], in_=th[:, part[0], :], func=ACT.Abs, scale=0.5)
+            stay(*part)
 
         out_view = out.rearrange("(mt p) c -> p mt c", p=P)
-        back_bank = (0, 3, 5)
-        out_banks = ((1, 2), (4, 0), (3, 1, 2, 6))
+        out_banks = ((0,), (1,), (2,), (3, 4, 5, 6))
 
         def quantize_w3():
             grouped = tile([P, N * PACK], BF16, "w3_grouped")
-            for mt in range(TILES):
-                nc.scalar.copy(
-                    out=grouped[:, mt * K_PASS : (mt + 1) * K_PASS].rearrange("p (c i j) -> p c j i", i=4, j=PACK),
-                    in_=w3_raw[:, :, mt * P : (mt + 1) * P].rearrange("p j (c i) -> p c j i", i=4),
-                )
-            return quantize(grouped[:], "w3")
+            nc.vector.tensor_copy(
+                out=grouped[:].rearrange("p (c i j) -> p c j i", i=4, j=PACK),
+                in_=w3_all[:].rearrange("p j (c i) -> p c j i", i=4),
+            )
+            return grouped
 
         def finish(n, w3q, zq):
             (w3_codes, w3_scales), (z_codes, z_scales) = w3q, zq
@@ -232,60 +211,72 @@ def tile_picked_advect_none_p_kernel(
                         stop=True,
                     )
                 result = tile([P, rows, width], F32, "result%d_%d" % (n, h))
-                copy_on("vector" if n == 2 and h % 2 == 1 else "scalar", result[:], acc[:])
-                queue = nc.scalar if n == 2 and h == 2 else nc.sync
+                copy_on("vector" if n == 3 and h % 2 == 0 else "scalar", result[:], acc[:])
+                queue = nc.scalar if n == 3 and h == 3 else nc.sync
                 queue.dma_start(out=out_view[:, rows * h : rows * (h + 1), cols], in_=result[:])
 
-        quantized = []
-        for n, (c0, width) in enumerate(CHUNKS):
-            cols = slice(c0, c0 + width)
-            blocks = range(c0 // P, (c0 + width) // P)
-            if n < 2:
-                d_west, d_east = differences(c0, width)
-                terms = tile([P, TILES * 2 * width], F32, "terms%d" % n)
-                view = terms[:].rearrange("p (t s c) -> p s t c", t=TILES, s=2)
-                for side, (op, d) in enumerate(((ALU.max, d_west), (ALU.min, d_east))):
-                    nc.vector.scalar_tensor_tensor(view[:, side], th[:, :, cols], 0.0, d, op, ALU.mult)
-                    for b in blocks:
-                        for t in range(TILES):
-                            add_turned(
-                                b, t, view[:, side, t, b * P - c0 : (b + 1) * P - c0],
-                                stop=(side == 1 and t == TILES - 1),
-                            )
-            else:
-                lists = slice(c0 // 16, (c0 + width) // 16)
-                leaving = tile([P, TILES, P], F32, "leaving")
-                for t in range(TILES):
-                    nc.vector.tensor_tensor(leaving[:, t, :], gates[:, 2, t, :], minus_half[t][:, cols], ALU.mult)
-                    add_turned(blocks[0], t, leaving[:, t, :])
-                for t in range(TILES):
-                    for side, neighbours in enumerate((west_sb, east_sb)):
-                        term = last_terms[t][:, side * P : (side + 1) * P]
-                        nc.vector.tensor_tensor(term, half[t][:].indirect(neighbours[:, lists]), gates[:, side, t, :], ALU.mult)
-                        add_turned(blocks[0], t, term, stop=(side == 1 and t == TILES - 1))
-                finish(1, w3q, quantized[1])
-            back = bank(back_bank[n], [P, len(blocks), 2, P])
-            for b in blocks:
-                zt = tile([P, H], BF16, "zt%d" % b)
-                copy_on(
-                    "vector" if b == BLOCKS - 1 else "scalar",
-                    zt[:].rearrange("c (g t r) -> c g t r", g=8, t=TILES),
-                    zt_acc[b][:].rearrange("c (t g r) -> c g t r", g=8, t=TILES),
-                )
-                words = zt[:].bitcast(F32)
-                for u in range(2):
-                    nc.tensor.transpose(back[:, b - blocks[0], u, :], words[:, u : H // 2 : 2], ident[:])
-            if n == 0:
-                z_words = last_terms[TILES - 1][:]
-            else:
-                z_words = tile([P, width * 2], F32, "z_words%d" % n)[:]
-            z_grouped = z_words.bitcast(BF16)
-            nc.scalar.copy(
-                out=z_words.rearrange("p (b r u) -> p b r u", u=2, r=P),
-                in_=back[:].rearrange("p b u r -> p b r u"),
+        from_west = [tile([P, TILES, w], F32, "from_west%d" % c) for c, w in CHUNKS]
+        from_east = [tile([P, TILES, w], F32, "from_east%d" % c) for c, w in EAST_CHUNKS]
+        z_grouped = [tile([P, w * PACK], BF16, "z_grouped%d" % c) for c, w in CHUNKS]
+
+        def fetch(terms, lists, c0, tiles=range(TILES)):
+            for t in tiles:
+                offsets = lists[:, c0 // 16 : (c0 + terms.shape[2]) // 16]
+                nc.scalar.activation(out=terms[:, t, :], in_=half[t][:].indirect(offsets), func=ACT.Copy)
+
+        def gate(dst, src, c0, op, tiles=slice(0, TILES)):
+            nc.vector.scalar_tensor_tensor(
+                dst[:, tiles, :], th[:, tiles, c0 : c0 + src.shape[2]], 0.0, src[:, tiles, :], op, ALU.mult
             )
-            quantized.append(quantize(z_grouped, "z%d" % n))
-            if n == 1:
-                w3q = quantize_w3()
-                finish(0, w3q, quantized[0])
-        finish(2, w3q, quantized[2])
+
+        def add_staying(dst, gated, c0):
+            nc.vector.tensor_tensor(dst, gated, staying[:, :, c0 : c0 + dst.shape[2]], ALU.add)
+
+        def round_z(dst, gained, lost):
+            nc.vector.tensor_tensor(
+                dst.rearrange("p (c i t) -> p c t i", i=2, t=TILES),
+                gained.rearrange("p t (c i) -> p c t i", i=2),
+                lost.rearrange("p t (c i) -> p c t i", i=2),
+                ALU.subtract,
+            )
+
+        west_terms = [terms[:] for terms in from_west]
+        east_terms = [terms[:] for terms in from_east]
+        w3_grouped = quantize_w3()
+        fetch(east_terms[0], east_sb, 0)
+        for t in range(FUSED):
+            nc.vector.tensor_tensor(from_west[0][:, t, :], half[t][:].indirect(west_sb[:, 0 : P // 16]), forward[:, t, :], ALU.mult)
+        fetch(east_terms[1], east_sb, 128)
+        fetch(west_terms[0], west_sb, 0, range(FUSED, TILES))
+        fetch(west_terms[1], west_sb, 128)
+        fetch(west_terms[2], west_sb, 256)
+        fetch(east_terms[2], east_sb, 384)
+        fetch(west_terms[3], west_sb, 384)
+        gate(east_terms[0], east_terms[0], 0, ALU.min)
+        w3q = quantize(w3_grouped[:], "w3")
+        add_staying(east_terms[0], east_terms[0], 0)
+        gated = tile([P, TILES, 2 * P], F32, "w3_grouped")[:]
+        gate(gated, east_terms[1], 128, ALU.min)
+        gate(west_terms[0], west_terms[0], 0, ALU.max, slice(FUSED, TILES))
+        add_staying(east_terms[1], gated, 128)
+        round_z(z_grouped[0][:], west_terms[0], east_terms[0])
+        gained1 = tile([P, TILES, P], F32, "gained1")[:]
+        gate(gained1, west_terms[1], 128, ALU.max)
+        finish(0, w3q, quantize(z_grouped[0][:], "z0"))
+        gained2 = tile([P, TILES, P], F32, "w3_grouped")[:]
+        gate(gained2, west_terms[2], 256, ALU.max)
+        round_z(z_grouped[1][:], gained1, east_terms[1][:, :, 0:P])
+        round_z(z_grouped[2][:], gained2, east_terms[1][:, :, P : 2 * P])
+        gated = tile([P, TILES, P], F32, "gained1")[:]
+        zq1 = quantize(z_grouped[1][:], "z1")
+        gate(gated, east_terms[2], 384, ALU.min)
+        finish(1, w3q, zq1)
+        finish(2, w3q, quantize(z_grouped[2][:], "z2"))
+        add_staying(east_terms[2], gated, 384)
+        gained3 = tile([P, TILES, P], F32, "z_grouped256")[:]
+        halves = (slice(0, P // 2), slice(P // 2, P))
+        for part in halves:
+            gate(gained3[:, :, part], west_terms[3][:, :, part], 384 + part.start, ALU.max)
+        for part in halves:
+            round_z(z_grouped[3][:, part.start * PACK : part.stop * PACK], gained3[:, :, part], east_terms[2][:, :, part])
+        finish(3, w3q, quantize(z_grouped[3][:], "z3"))

@@ -66,14 +66,19 @@ def tile_picked_advect_none_p_kernel(
                 nc.sync.dma_start(out=parts[h][:], in_=rows[:, :, h * H // 2 : (h + 1) * H // 2])
             return parts
 
+        def load_scale_rows(rows):
+            for r in rows:
+                for z in range(PASSES):
+                    nc.sync.dma_start(
+                        out=scale_table[4 * z + r : P : 32, :].bitcast(I32),
+                        in_=x_scales[z, r : 16 : 4, :].bitcast(I32),
+                    )
+
         load_words(0)
         nc.sync.dma_start(offs_sb[:], offs)
-        for q in range(4):
-            nc.sync.dma_start(
-                out=scale_table[32 * q : 32 * q + 4 * PASSES, :].bitcast(I32),
-                in_=x_scales[:, 4 * q : 4 * q + 4, :].bitcast(I32),
-            )
+        load_scale_rows(range(0, 2))
         w2_raw = [load_rows(w2, 0, "w2_raw0")]
+        load_scale_rows(range(2, 4))
         load_words(1)
         w2_raw.append(load_halves(w2, 1, "w2_raw1"))
         w1_raw = [load_rows(w1, 0, "w1_raw0"), load_halves(w1, 1, "w1_raw1")]

@@ -59,11 +59,13 @@ def tile_picked_advect_none_p_kernel(
             )
             return raw
 
-        def load_halves(w, z, name):
+        def load_parts(w, z, name, widths=(H // 2, H // 2)):
             rows = w[z * K_PASS : (z + 1) * K_PASS, :].rearrange("(p j) c -> p j c", j=PACK)
-            parts = [tile([P, PACK, H // 2], F32, "%s_%d" % (name, h)) for h in range(2)]
-            for h in range(2):
-                nc.sync.dma_start(out=parts[h][:], in_=rows[:, :, h * H // 2 : (h + 1) * H // 2])
+            parts, first = [], 0
+            for h, width in enumerate(widths):
+                parts.append(tile([P, PACK, width], F32, "%s_%d" % (name, h)))
+                nc.sync.dma_start(out=parts[h][:], in_=rows[:, :, first : first + width])
+                first = first + width
             return parts
 
         def load_scale_rows(rows):
@@ -74,14 +76,14 @@ def tile_picked_advect_none_p_kernel(
                         in_=x_scales[z, r : 16 : 4, :].bitcast(I32),
                     )
 
-        load_words(0)
+        w2_raw = [load_rows(w2, 0, "w2_raw0")]
         nc.sync.dma_start(offs_sb[:], offs)
         load_scale_rows(range(0, 2))
-        w2_raw = [load_rows(w2, 0, "w2_raw0")]
+        load_words(0)
         load_scale_rows(range(2, 4))
+        w2_raw.append(load_rows(w2, 1, "w2_raw1"))
         load_words(1)
-        w2_raw.append(load_halves(w2, 1, "w2_raw1"))
-        w1_raw = [load_rows(w1, 0, "w1_raw0"), load_halves(w1, 1, "w1_raw1")]
+        w1_raw = [load_rows(w1, 0, "w1_raw0"), load_parts(w1, 1, "w1_raw1")]
         w3_all = load_rows(w3, 0, "w3_all")
         nc.sync.dma_start(east_sb[:], east)
         nc.sync.dma_start(west_sb[:], west)
@@ -120,50 +122,54 @@ def tile_picked_advect_none_p_kernel(
                     pairs.append((codes[:, u * P : (u + 1) * P], scales[:, u * P : (u + 1) * P]))
             return pairs
 
-        x_codes = [tile([P, S], U32, "x_codes%d" % z) for z in range(PASSES)]
+        x_codes = [tile([P, S], U32, "x_codes0")]
         x_scale = tile([P, S], U8, "x_scale")
 
-        def gather_words(z):
-            nc.vector.tensor_copy(out=x_codes[z][:], in_=word_table[z][:].bitcast(U32).indirect(offs_sb[:]))
+        def gather_words(z, cells=slice(0, S)):
+            offsets = offs_sb[:, cells.start // 16 : cells.stop // 16]
+            nc.vector.tensor_copy(out=x_codes[z][:, cells], in_=word_table[z][:].bitcast(U32).indirect(offsets))
 
-        def product(acc, wq, z, cells=slice(0, S)):
+        def product(acc, wq, z, cells=slice(0, S), opens=True, closes=True):
             codes, scales = wq
             nc.tensor.matmul_mx(
-                out=acc[:],
+                out=acc,
                 lhsT=codes.bitcast(FP8X4),
                 lhsT_scale=scales,
                 rhs=x_codes[z][:, cells].bitcast(FP8X4),
                 rhs_scale=x_scale[4 * z : P, cells],
-                start=(z == 0),
-                stop=(z == PASSES - 1),
+                start=(z == 0 and opens),
+                stop=(z == PASSES - 1 and closes),
             )
 
+        w2q = quantize_pass((("vector", w2_raw[0][:]),), "w2p0", 2)
         gather_words(0)
         nc.vector.tensor_copy(out=x_scale[:], in_=scale_table[:].indirect(offs_sb[:]))
-        c_acc = [bank(t, [P, S]) for t in range(TILES)]
-        w2q = quantize_pass((("vector", w2_raw[0][:]),), "w2p0", 2)
-        for t in range(TILES):
-            product(c_acc[t], w2q[t], 0)
-        gather_words(1)
-        w2q = quantize_pass(
-            (("scalar", w2_raw[1][0][:]), ("vector", w2_raw[1][1][:])),
-            "w2p1",
-            1,
-        )
+        low, high = slice(0, S // 2), slice(S // 2, S)
+        c_parts = [(u, cells, bank(2 * h + u, [P, 2, S // 2])) for h, cells in enumerate((low, high)) for u in range(2)]
+
+        def speeds_pass(wq, z, parts):
+            for u, cells, acc in parts:
+                for n in range(2):
+                    product(acc[:, n, :], wq[2 * u + n], z, cells, n == 0, n == 1)
+
+        speeds_pass(w2q, 0, c_parts)
+        w2q = quantize_pass((("vector", w2_raw[1][:]),), "w2p1", 2)
+        x_codes.append(tile([P, S], U32, "w2p1_g"))
         th = tile([P, TILES, S], F32, "th")
         speed = tile([P, TILES, S], F32, "speed")
-        for t in range(TILES):
-            product(c_acc[t], w2q[t], 1)
-            nc.scalar.activation(out=th[:, t, :], in_=c_acc[t][:], func=ACT.Tanh)
+        for h, cells in enumerate((low, high)):
+            gather_words(1, cells)
+            speeds_pass(w2q, 1, c_parts[2 * h : 2 * h + 2])
+        for u, cells, acc in c_parts:
+            nc.scalar.activation(out=th[:, 2 * u : 2 * u + 2, cells], in_=acc[:], func=ACT.Tanh)
 
         nc.scalar.activation(out=speed[:, 0, :], in_=th[:, 0, :], func=ACT.Abs, scale=0.5)
 
-        low, high = slice(0, S // 2), slice(S // 2, S)
         y_parts = [(0, low, bank(TILES, [P, S // 2])), (0, high, bank(0, [P, S // 2]))]
         y_parts.extend((t, slice(0, S), bank(TILES + t, [P, S])) for t in range(1, TILES))
         w1q = quantize_pass((("vector", w1_raw[0][:]),), "w1p0", 4)
         for t, cells, acc in y_parts:
-            product(acc, w1q[t], 0, cells)
+            product(acc[:], w1q[t], 0, cells)
         w1q = quantize_pass((("vector", w1_raw[1][0][:]), ("vector", w1_raw[1][1][:])), "w1p1", 1)
         forward = tile([P, FUSED, P], F32, "w1p1_g")
         nc.vector.tensor_scalar_max(forward[:], th[:, 0:FUSED, 0:P], 0.0)
@@ -177,7 +183,7 @@ def tile_picked_advect_none_p_kernel(
             nc.vector.scalar_tensor_tensor(staying[:, t, cells], speed[:, t, cells], 1.0, acc[:], ALU.subtract, ALU.mult)
 
         for t, cells, acc in y_parts:
-            product(acc, w1q[t], 1, cells)
+            product(acc[:], w1q[t], 1, cells)
         stay(*y_parts[1])
         for part in y_parts:
             copy_half(*part)
@@ -187,7 +193,7 @@ def tile_picked_advect_none_p_kernel(
             stay(*part)
 
         out_view = out.rearrange("(mt p) c -> p mt c", p=P)
-        out_banks = ((0,), (1,), (2,), (3, 4, 5, 6))
+        out_banks = ((0,), (1, 2), (3, 4, 5, 6))
 
         def quantize_w3():
             grouped = tile([P, N * PACK], BF16, "w3_grouped")
@@ -199,7 +205,7 @@ def tile_picked_advect_none_p_kernel(
 
         def finish(n, w3q, zq):
             (w3_codes, w3_scales), (z_codes, z_scales) = w3q, zq
-            c0, width = CHUNKS[n]
+            c0, width = EAST_CHUNKS[n]
             cols = slice(c0, c0 + width)
             rows = TILES // len(out_banks[n])
             for h, index in enumerate(out_banks[n]):
@@ -216,13 +222,13 @@ def tile_picked_advect_none_p_kernel(
                         stop=True,
                     )
                 result = tile([P, rows, width], F32, "result%d_%d" % (n, h))
-                copy_on("vector" if n == 3 and h % 2 == 0 else "scalar", result[:], acc[:])
-                queue = nc.scalar if n == 3 and h == 3 else nc.sync
+                copy_on("vector" if n == 2 and h % 2 == 0 else "scalar", result[:], acc[:])
+                queue = nc.scalar if n > 0 and h == len(out_banks[n]) - 1 else nc.sync
                 queue.dma_start(out=out_view[:, rows * h : rows * (h + 1), cols], in_=result[:])
 
         from_west = [tile([P, TILES, w], F32, "from_west%d" % c) for c, w in CHUNKS]
         from_east = [tile([P, TILES, w], F32, "from_east%d" % c) for c, w in EAST_CHUNKS]
-        z_grouped = [tile([P, w * PACK], BF16, "z_grouped%d" % c) for c, w in CHUNKS]
+        z_grouped = [tile([P, w * PACK], BF16, "z_grouped%d" % c) for c, w in EAST_CHUNKS]
 
         def fetch(terms, lists, c0, tiles=range(TILES)):
             for t in tiles:
@@ -270,18 +276,16 @@ def tile_picked_advect_none_p_kernel(
         finish(0, w3q, quantize(z_grouped[0][:], "z0"))
         gained2 = tile([P, TILES, P], F32, "w3_grouped")[:]
         gate(gained2, west_terms[2], 256, ALU.max)
-        round_z(z_grouped[1][:], gained1, east_terms[1][:, :, 0:P])
-        round_z(z_grouped[2][:], gained2, east_terms[1][:, :, P : 2 * P])
+        round_z(z_grouped[1][:, 0 : P * PACK], gained1, east_terms[1][:, :, 0:P])
+        round_z(z_grouped[1][:, P * PACK :], gained2, east_terms[1][:, :, P : 2 * P])
         gated = tile([P, TILES, P], F32, "gained1")[:]
-        zq1 = quantize(z_grouped[1][:], "z1")
         gate(gated, east_terms[2], 384, ALU.min)
-        finish(1, w3q, zq1)
-        finish(2, w3q, quantize(z_grouped[2][:], "z2"))
+        finish(1, w3q, quantize(z_grouped[1][:], "z1"))
         add_staying(east_terms[2], gated, 384)
-        gained3 = tile([P, TILES, P], F32, "z_grouped256")[:]
+        gained3 = tile([P, TILES, P], F32, "z_grouped128")[:]
         halves = (slice(0, P // 2), slice(P // 2, P))
         for part in halves:
             gate(gained3[:, :, part], west_terms[3][:, :, part], 384 + part.start, ALU.max)
         for part in halves:
-            round_z(z_grouped[3][:, part.start * PACK : part.stop * PACK], gained3[:, :, part], east_terms[2][:, :, part])
-        finish(3, w3q, quantize(z_grouped[3][:], "z3"))
+            round_z(z_grouped[2][:, part.start * PACK : part.stop * PACK], gained3[:, :, part], east_terms[2][:, :, part])
+        finish(2, w3q, quantize(z_grouped[2][:], "z2"))

@@ -1,6 +1,7 @@
 from contextlib import ExitStack
 
 import concourse.mybir as mybir
+from concourse.masks import make_identity
 
 K, T, S, N, H = 1024, 2048, 512, 512, 512
 FLOPS = 2 * (2 * K * H * S + H * N * S)
@@ -20,9 +21,10 @@ PACK = 4
 K_PASS = P * PACK
 PASSES = K // K_PASS
 TILES = H // P
-FUSED = 2
-CHUNKS = ((0, 128), (128, 128), (256, 128), (384, 128))
-EAST_CHUNKS = ((0, 128), (128, 256), (384, 128))
+CHUNKS = S // P
+WEST_PIECES = ((0, 256), (256, 128), (384, 128))
+OUT_CHUNKS = WEST_PIECES
+WORD_PIECES = (slice(0, 128), slice(128, 256), slice(256, 512))
 
 
 def tile_picked_advect_none_p_kernel(
@@ -44,6 +46,9 @@ def tile_picked_advect_none_p_kernel(
         east_sb = sb.tile([P, S // 16], U16, name="east_sb")
         scale_table = tile([P, T], U8, "scale_table")
         nc.gpsimd.memset(scale_table[:].bitcast(I32), 0)
+
+        identity = tile([P, P], F32, "identity")
+        make_identity(nc, identity[:])
 
         word_table = [tile([P, T], I32, "word_table%d" % z) for z in range(PASSES)]
 
@@ -141,71 +146,96 @@ def tile_picked_advect_none_p_kernel(
                 stop=(z == PASSES - 1 and closes),
             )
 
-        w2q = quantize_pass((("vector", w2_raw[0][:]),), "w2p0", 2)
+        def round_pass(raws, name):
+            grouped = tile([P, TILES, K_PASS], BF16, name + "_g")
+            first = 0
+            for raw in raws:
+                cast("vector", grouped, first, raw)
+                first = first + raw.shape[2]
+            return grouped
+
+        def chunk(n):
+            return slice(n * P, (n + 1) * P)
+
+        def speeds_pass(wq, z, chunks):
+            codes, scales = wq
+            for n in chunks:
+                nc.tensor.matmul_mx(
+                    out=u_banks[n][:],
+                    lhsT=x_codes[z][:, chunk(n)].bitcast(FP8X4),
+                    lhsT_scale=x_scale[4 * z : P, chunk(n)],
+                    rhs=codes[:].bitcast(FP8X4),
+                    rhs_scale=scales[:],
+                    start=(z == 0),
+                    stop=(z == PASSES - 1),
+                )
+
+        u_banks = [bank(n, [P, H]) for n in range(CHUNKS)]
+        w2q = quantize(round_pass([w2_raw[0][:]], "w2p0")[:].rearrange("p t c -> p (t c)"), "w2p0")
         gather_words(0)
         nc.vector.tensor_copy(out=x_scale[:], in_=scale_table[:].indirect(offs_sb[:]))
-        low, high = slice(0, S // 2), slice(S // 2, S)
-        c_parts = [(u, cells, bank(2 * h + u, [P, 2, S // 2])) for h, cells in enumerate((low, high)) for u in range(2)]
-
-        def speeds_pass(wq, z, parts):
-            for u, cells, acc in parts:
-                for n in range(2):
-                    product(acc[:, n, :], wq[2 * u + n], z, cells, n == 0, n == 1)
-
-        speeds_pass(w2q, 0, c_parts)
-        w2q = quantize_pass((("vector", w2_raw[1][:]),), "w2p1", 2)
+        speeds_pass(w2q, 0, range(CHUNKS))
+        w2q = quantize(round_pass([w2_raw[1][:]], "w2p1")[:].rearrange("p t c -> p (t c)"), "w2p1")
         x_codes.append(tile([P, S], U32, "w2p1_g"))
-        th = tile([P, TILES, S], F32, "th")
-        speed = tile([P, TILES, S], F32, "speed")
-        for h, cells in enumerate((low, high)):
+        for cells in WORD_PIECES:
             gather_words(1, cells)
-            speeds_pass(w2q, 1, c_parts[2 * h : 2 * h + 2])
-        for u, cells, acc in c_parts:
-            nc.scalar.activation(out=th[:, 2 * u : 2 * u + 2, cells], in_=acc[:], func=ACT.Tanh)
+            speeds_pass(w2q, 1, range(cells.start // P, cells.stop // P))
+        th_cells = [tile([P, H], F32, "th_cells%d" % n) for n in range(CHUNKS)]
+        th = [bank(CHUNKS + n, [P, TILES, P]) for n in range(CHUNKS)]
+        speed = tile([P, CHUNKS, TILES, P], F32, "speed")
+        for n in range(CHUNKS):
+            nc.scalar.activation(out=th_cells[n][:], in_=u_banks[n][:], func=ACT.Tanh)
+            for t in range(TILES):
+                nc.tensor.transpose(th[n][:, t, :], th_cells[n][:, t * P : (t + 1) * P], identity[:])
+        for n in range(CHUNKS):
+            nc.scalar.activation(out=speed[:, n], in_=th[n][:], func=ACT.Abs, scale=0.5)
 
-        nc.scalar.activation(out=speed[:, 0, :], in_=th[:, 0, :], func=ACT.Abs, scale=0.5)
-
-        y_parts = [(0, low, bank(TILES, [P, S // 2])), (0, high, bank(0, [P, S // 2]))]
-        y_parts.extend((t, slice(0, S), bank(TILES + t, [P, S])) for t in range(1, TILES))
+        y_banks = [bank(t, [P, S]) for t in range(TILES)]
         w1q = quantize_pass((("vector", w1_raw[0][:]),), "w1p0", 4)
-        for t, cells, acc in y_parts:
-            product(acc[:], w1q[t], 0, cells)
+        for t in range(TILES):
+            product(y_banks[t][:], w1q[t], 0)
         w1q = quantize_pass((("vector", w1_raw[1][0][:]), ("vector", w1_raw[1][1][:])), "w1p1", 1)
-        forward = tile([P, FUSED, P], F32, "w1p1_g")
-        nc.vector.tensor_scalar_max(forward[:], th[:, 0:FUSED, 0:P], 0.0)
+        for t in range(TILES):
+            product(y_banks[t][:], w1q[t], 1)
+
+        w3_grouped = tile([P, N, PACK], BF16, "w1p1_g")
+        nc.gpsimd.tensor_scalar(w3_grouped[:], w3_all[:].rearrange("p j c -> p c j"), 1.0, 0.0, ALU.mult, ALU.add)
+
         half = [tile([P, S], F32, "half%d" % t) for t in range(TILES)]
-        staying = tile([P, TILES, S], F32, "staying")
+        staying = tile([P, CHUNKS, TILES, P], F32, "staying")
+        from_west = [tile([P, TILES, w], F32, "from_west%d" % c) for c, w in WEST_PIECES]
+        from_east = [tile([P, TILES, 2 * P], F32, "from_east%d" % h) for h in range(2)]
 
-        def copy_half(t, cells, acc):
-            nc.scalar.activation(out=half[t][:, cells], in_=acc[:], func=ACT.Copy, scale=0.5)
+        def stay(t):
+            nc.vector.scalar_tensor_tensor(
+                staying[:, :, t, :], speed[:, :, t, :], 1.0, y_banks[t][:].rearrange("p (n c) -> p n c", c=P), ALU.subtract, ALU.mult
+            )
 
-        def stay(t, cells, acc):
-            nc.vector.scalar_tensor_tensor(staying[:, t, cells], speed[:, t, cells], 1.0, acc[:], ALU.subtract, ALU.mult)
+        def fetch(terms, lists, c0, tiles=range(TILES)):
+            for t in tiles:
+                offsets = lists[:, c0 // 16 : (c0 + terms.shape[2]) // 16]
+                nc.scalar.activation(out=terms[:, t, :], in_=half[t][:].indirect(offsets), func=ACT.Copy)
 
-        for t, cells, acc in y_parts:
-            product(acc[:], w1q[t], 1, cells)
-        stay(*y_parts[1])
-        for part in y_parts:
-            copy_half(*part)
-        stay(*y_parts[0])
-        for part in y_parts[2:]:
-            nc.scalar.activation(out=speed[:, part[0], :], in_=th[:, part[0], :], func=ACT.Abs, scale=0.5)
-            stay(*part)
+        nc.scalar.activation(out=half[0][:], in_=y_banks[0][:], func=ACT.Copy, scale=0.5)
+        nc.vector.tensor_scalar_mul(half[1][:], y_banks[1][:], 0.5)
+        fetch(from_east[0], east_sb, 0, range(0, 1))
+        stay(0)
+        nc.scalar.activation(out=half[2][:], in_=y_banks[2][:], func=ACT.Copy, scale=0.5)
+        nc.vector.tensor_scalar_mul(half[3][:], y_banks[3][:], 0.5)
+        for t in range(1, TILES):
+            stay(t)
+        fetch(from_east[0], east_sb, 0, range(1, TILES))
+        fetch(from_west[0], west_sb, 0)
+        fetch(from_east[1], east_sb, 2 * P)
+        fetch(from_west[1], west_sb, 2 * P)
+        fetch(from_west[2], west_sb, 3 * P)
 
         out_view = out.rearrange("(mt p) c -> p mt c", p=P)
-        out_banks = ((0,), (1, 2), (3, 4, 5, 6))
-
-        def quantize_w3():
-            grouped = tile([P, N * PACK], BF16, "w3_grouped")
-            nc.vector.tensor_copy(
-                out=grouped[:].rearrange("p (c i j) -> p c j i", i=4, j=PACK),
-                in_=w3_all[:].rearrange("p j (c i) -> p c j i", i=4),
-            )
-            return grouped
+        out_banks = ((0, 1), (2,), (3, 4, 5, 6))
 
         def finish(n, w3q, zq):
             (w3_codes, w3_scales), (z_codes, z_scales) = w3q, zq
-            c0, width = EAST_CHUNKS[n]
+            c0, width = OUT_CHUNKS[n]
             cols = slice(c0, c0 + width)
             rows = TILES // len(out_banks[n])
             for h, index in enumerate(out_banks[n]):
@@ -223,25 +253,14 @@ def tile_picked_advect_none_p_kernel(
                     )
                 result = tile([P, rows, width], F32, "result%d_%d" % (n, h))
                 copy_on("vector" if n == 2 and h % 2 == 0 else "scalar", result[:], acc[:])
-                queue = nc.scalar if n > 0 and h == len(out_banks[n]) - 1 else nc.sync
+                queue = nc.scalar if n == 2 and h == len(out_banks[n]) - 1 else nc.sync
                 queue.dma_start(out=out_view[:, rows * h : rows * (h + 1), cols], in_=result[:])
 
-        from_west = [tile([P, TILES, w], F32, "from_west%d" % c) for c, w in CHUNKS]
-        from_east = [tile([P, TILES, w], F32, "from_east%d" % c) for c, w in EAST_CHUNKS]
-        z_grouped = [tile([P, w * PACK], BF16, "z_grouped%d" % c) for c, w in EAST_CHUNKS]
+        def gate(dst, n, src, op, part=slice(0, P)):
+            nc.vector.scalar_tensor_tensor(dst[:, :, part], th[n][:, :, part], 0.0, src[:, :, part], op, ALU.mult)
 
-        def fetch(terms, lists, c0, tiles=range(TILES)):
-            for t in tiles:
-                offsets = lists[:, c0 // 16 : (c0 + terms.shape[2]) // 16]
-                nc.scalar.activation(out=terms[:, t, :], in_=half[t][:].indirect(offsets), func=ACT.Copy)
-
-        def gate(dst, src, c0, op, tiles=slice(0, TILES)):
-            nc.vector.scalar_tensor_tensor(
-                dst[:, tiles, :], th[:, tiles, c0 : c0 + src.shape[2]], 0.0, src[:, tiles, :], op, ALU.mult
-            )
-
-        def add_staying(dst, gated, c0):
-            nc.vector.tensor_tensor(dst, gated, staying[:, :, c0 : c0 + dst.shape[2]], ALU.add)
+        def add_staying(dst, n, gated):
+            nc.vector.tensor_tensor(dst, gated, staying[:, n], ALU.add)
 
         def round_z(dst, gained, lost):
             nc.vector.tensor_tensor(
@@ -251,41 +270,40 @@ def tile_picked_advect_none_p_kernel(
                 ALU.subtract,
             )
 
-        west_terms = [terms[:] for terms in from_west]
-        east_terms = [terms[:] for terms in from_east]
-        w3_grouped = quantize_w3()
-        fetch(east_terms[0], east_sb, 0)
-        for t in range(FUSED):
-            nc.vector.tensor_tensor(from_west[0][:, t, :], half[t][:].indirect(west_sb[:, 0 : P // 16]), forward[:, t, :], ALU.mult)
-        fetch(east_terms[1], east_sb, 128)
-        fetch(west_terms[0], west_sb, 0, range(FUSED, TILES))
-        fetch(west_terms[1], west_sb, 128)
-        fetch(west_terms[2], west_sb, 256)
-        fetch(east_terms[2], east_sb, 384)
-        fetch(west_terms[3], west_sb, 384)
-        gate(east_terms[0], east_terms[0], 0, ALU.min)
-        w3q = quantize(w3_grouped[:], "w3")
-        add_staying(east_terms[0], east_terms[0], 0)
-        gated = tile([P, TILES, 2 * P], F32, "w3_grouped")[:]
-        gate(gated, east_terms[1], 128, ALU.min)
-        gate(west_terms[0], west_terms[0], 0, ALU.max, slice(FUSED, TILES))
-        add_staying(east_terms[1], gated, 128)
-        round_z(z_grouped[0][:], west_terms[0], east_terms[0])
-        gained1 = tile([P, TILES, P], F32, "gained1")[:]
-        gate(gained1, west_terms[1], 128, ALU.max)
-        finish(0, w3q, quantize(z_grouped[0][:], "z0"))
-        gained2 = tile([P, TILES, P], F32, "w3_grouped")[:]
-        gate(gained2, west_terms[2], 256, ALU.max)
-        round_z(z_grouped[1][:, 0 : P * PACK], gained1, east_terms[1][:, :, 0:P])
-        round_z(z_grouped[1][:, P * PACK :], gained2, east_terms[1][:, :, P : 2 * P])
-        gated = tile([P, TILES, P], F32, "gained1")[:]
-        gate(gated, east_terms[2], 384, ALU.min)
-        finish(1, w3q, quantize(z_grouped[1][:], "z1"))
-        add_staying(east_terms[2], gated, 384)
-        gained3 = tile([P, TILES, P], F32, "z_grouped128")[:]
-        halves = (slice(0, P // 2), slice(P // 2, P))
-        for part in halves:
-            gate(gained3[:, :, part], west_terms[3][:, :, part], 384 + part.start, ALU.max)
-        for part in halves:
-            round_z(z_grouped[2][:, part.start * PACK : part.stop * PACK], gained3[:, :, part], east_terms[2][:, :, part])
-        finish(2, w3q, quantize(z_grouped[2][:], "z2"))
+        z_grouped = [tile([P, w * PACK], BF16, "z_grouped%d" % c) for c, w in OUT_CHUNKS]
+        w3q = quantize(w3_grouped[:].rearrange("p c j -> p (c j)"), "w3")
+        low, high = slice(0, P), slice(P, 2 * P)
+
+        def add_on_gpsimd(n, gated):
+            lost = tile([P, TILES, P], F32, "lost%d" % n)[:]
+            nc.gpsimd.tensor_tensor(lost, gated, staying[:, n], ALU.add)
+            return lost
+
+        def leave(n):
+            finish(n, w3q, quantize(z_grouped[n][:], "z%d" % n))
+
+        gated = tile([P, 2, TILES, P], F32, "w1p1_g")
+        lost = []
+        for n, part in enumerate((low, high)):
+            gate(gated[:, n], n, from_east[0][:, :, part], ALU.min)
+            lost.append(add_on_gpsimd(n, gated[:, n]))
+        gained = tile([P, 2, TILES, P], F32, "from_east0")
+        for n, part in enumerate((low, high)):
+            gate(gained[:, n], n, from_west[0][:, :, part], ALU.max)
+        for n in range(2):
+            round_z(z_grouped[0][:, n * P * PACK : (n + 1) * P * PACK], gained[:, n], lost[n])
+        gated = tile([P, 2, TILES, P], F32, "from_east0")
+        gate(gated[:, 0], 2, from_east[1][:, :, low], ALU.min)
+        lost = add_on_gpsimd(2, gated[:, 0])
+        leave(0)
+        gate(gated[:, 1], 3, from_east[1][:, :, high], ALU.min)
+        gained = tile([P, TILES, P], F32, "z_grouped0")[:]
+        gate(gained, 2, from_west[1][:], ALU.max)
+        round_z(z_grouped[1][:], gained, lost)
+        lost = tile([P, TILES, P], F32, "lost2")[:]
+        add_staying(lost, 3, gated[:, 1])
+        gained = tile([P, TILES, P], F32, "z_grouped0")[:]
+        gate(gained, 3, from_west[2][:], ALU.max)
+        leave(1)
+        round_z(z_grouped[2][:], gained, lost)
+        leave(2)

@@ -22,8 +22,7 @@ K_PASS = P * PACK
 PASSES = K // K_PASS
 TILES = H // P
 CHUNKS = S // P
-WEST_PIECES = ((0, 256), (256, 128), (384, 128))
-OUT_CHUNKS = WEST_PIECES
+OUT_CHUNKS = ((0, 256), (256, 128), (384, 128))
 WORD_PIECES = (slice(0, 128), slice(128, 256), slice(256, 512))
 
 
@@ -181,14 +180,19 @@ def tile_picked_advect_none_p_kernel(
             gather_words(1, cells)
             speeds_pass(w2q, 1, range(cells.start // P, cells.stop // P))
         th_cells = [tile([P, H], F32, "th_cells%d" % n) for n in range(CHUNKS)]
-        th = [bank(CHUNKS + n, [P, TILES, P]) for n in range(CHUNKS)]
-        speed = tile([P, CHUNKS, TILES, P], F32, "speed")
+        th = [[bank(CHUNKS + 2 * u + h, [P, 2, S // 2]) for h in range(2)] for u in range(2)]
+        speed = tile([P, TILES, S], F32, "speed")
         for n in range(CHUNKS):
             nc.scalar.activation(out=th_cells[n][:], in_=u_banks[n][:], func=ACT.Tanh)
             for t in range(TILES):
-                nc.tensor.transpose(th[n][:, t, :], th_cells[n][:, t * P : (t + 1) * P], identity[:])
-        for n in range(CHUNKS):
-            nc.scalar.activation(out=speed[:, n], in_=th[n][:], func=ACT.Abs, scale=0.5)
+                nc.tensor.transpose(
+                    th[t // 2][n // 2][:, t % 2, chunk(n % 2)], th_cells[n][:, t * P : (t + 1) * P], identity[:]
+                )
+        pairs = (slice(0, 2), slice(2, 4))
+        halves = (slice(0, S // 2), slice(S // 2, S))
+        for u in range(2):
+            for h in range(2):
+                nc.scalar.activation(out=speed[:, pairs[u], halves[h]], in_=th[u][h][:], func=ACT.Abs, scale=0.5)
 
         y_banks = [bank(t, [P, S]) for t in range(TILES)]
         w1q = quantize_pass((("vector", w1_raw[0][:]),), "w1p0", 4)
@@ -202,44 +206,38 @@ def tile_picked_advect_none_p_kernel(
         nc.gpsimd.tensor_scalar(w3_grouped[:], w3_all[:].rearrange("p j c -> p c j"), 1.0, 0.0, ALU.mult, ALU.add)
 
         half = [tile([P, S], F32, "half%d" % t) for t in range(TILES)]
-        staying = tile([P, CHUNKS, TILES, P], F32, "staying")
-        from_west = [tile([P, TILES, w], F32, "from_west%d" % c) for c, w in WEST_PIECES]
-        from_east = [tile([P, TILES, 2 * P], F32, "from_east%d" % h) for h in range(2)]
+        from_east = [[tile([P, 2, S // 2], F32, "from_east%d%d" % (u, h)) for h in range(2)] for u in range(2)]
+        from_west = [[tile([P, 2, w], F32, "from_west%d_%d" % (u, c)) for c, w in OUT_CHUNKS] for u in range(2)]
 
-        def stay(t):
-            nc.vector.scalar_tensor_tensor(
-                staying[:, :, t, :], speed[:, :, t, :], 1.0, y_banks[t][:].rearrange("p (n c) -> p n c", c=P), ALU.subtract, ALU.mult
-            )
-
-        def fetch(terms, lists, c0, tiles=range(TILES)):
-            for t in tiles:
+        def fetch(terms, lists, u, c0):
+            for n in range(2):
                 offsets = lists[:, c0 // 16 : (c0 + terms.shape[2]) // 16]
-                nc.scalar.activation(out=terms[:, t, :], in_=half[t][:].indirect(offsets), func=ACT.Copy)
+                nc.scalar.activation(out=terms[:, n, :], in_=half[2 * u + n][:].indirect(offsets), func=ACT.Copy)
 
         nc.scalar.activation(out=half[0][:], in_=y_banks[0][:], func=ACT.Copy, scale=0.5)
-        nc.vector.tensor_scalar_mul(half[1][:], y_banks[1][:], 0.5)
-        fetch(from_east[0], east_sb, 0, range(0, 1))
-        stay(0)
-        nc.scalar.activation(out=half[2][:], in_=y_banks[2][:], func=ACT.Copy, scale=0.5)
-        nc.vector.tensor_scalar_mul(half[3][:], y_banks[3][:], 0.5)
         for t in range(1, TILES):
-            stay(t)
-        fetch(from_east[0], east_sb, 0, range(1, TILES))
-        fetch(from_west[0], west_sb, 0)
-        fetch(from_east[1], east_sb, 2 * P)
-        fetch(from_west[1], west_sb, 2 * P)
-        fetch(from_west[2], west_sb, 3 * P)
+            nc.vector.tensor_scalar_mul(half[t][:], y_banks[t][:], 0.5)
+        for u in range(2):
+            fetch(from_east[u][0], east_sb, u, 0)
+            fetch(from_west[u][0], west_sb, u, 0)
+        for u in range(2):
+            fetch(from_east[u][1], east_sb, u, S // 2)
+        for n in range(1, 3):
+            for u in range(2):
+                fetch(from_west[u][n], west_sb, u, OUT_CHUNKS[n][0])
 
         out_view = out.rearrange("(mt p) c -> p mt c", p=P)
-        out_banks = ((0, 1), (2,), (3, 4, 5, 6))
+        out_banks = ((0, 1), (2, 3), (4, 6, 5, 7))
 
-        def finish(n, w3q, zq):
+        def multiply(n, w3q, zq):
             (w3_codes, w3_scales), (z_codes, z_scales) = w3q, zq
             c0, width = OUT_CHUNKS[n]
             cols = slice(c0, c0 + width)
             rows = TILES // len(out_banks[n])
+            accs = []
             for h, index in enumerate(out_banks[n]):
                 acc = bank(index, [P, rows, width])
+                accs.append((acc, out_view[:, rows * h : rows * (h + 1), cols]))
                 for m in range(rows):
                     mt = rows * h + m
                     nc.tensor.matmul_mx(
@@ -251,16 +249,35 @@ def tile_picked_advect_none_p_kernel(
                         start=True,
                         stop=True,
                     )
-                result = tile([P, rows, width], F32, "result%d_%d" % (n, h))
-                copy_on("vector" if n == 2 and h % 2 == 0 else "scalar", result[:], acc[:])
-                queue = nc.scalar if n == 2 and h == len(out_banks[n]) - 1 else nc.sync
-                queue.dma_start(out=out_view[:, rows * h : rows * (h + 1), cols], in_=result[:])
+            return accs
 
-        def gate(dst, n, src, op, part=slice(0, P)):
-            nc.vector.scalar_tensor_tensor(dst[:, :, part], th[n][:, :, part], 0.0, src[:, :, part], op, ALU.mult)
+        def store(engine, queue, name, acc, dst):
+            result = tile(list(acc.shape), F32, name)
+            copy_on(engine, result[:], acc[:])
+            queue.dma_start(out=dst, in_=result[:])
 
-        def add_staying(dst, n, gated):
-            nc.vector.tensor_tensor(dst, gated, staying[:, n], ALU.add)
+        staying = tile([P, TILES, S], F32, "staying")
+
+        def stay(t):
+            nc.vector.scalar_tensor_tensor(staying[:, t, :], speed[:, t, :], 1.0, y_banks[t][:], ALU.subtract, ALU.mult)
+
+        def gate_east(gated, u, h):
+            nc.vector.scalar_tensor_tensor(gated, th[u][h][:], 0.0, from_east[u][h][:], ALU.min, ALU.mult)
+
+        def add_staying(lost, gated, u, h):
+            nc.gpsimd.tensor_tensor(lost[:, pairs[u], :], gated, staying[:, pairs[u], halves[h]], ALU.add)
+
+        def gate_west(dst, u, n):
+            c0, width = OUT_CHUNKS[n]
+            first = c0 % (S // 2)
+            nc.vector.scalar_tensor_tensor(
+                dst[:, pairs[u], first : first + width],
+                th[u][c0 // (S // 2)][:, :, first : first + width],
+                0.0,
+                from_west[u][n][:],
+                ALU.max,
+                ALU.mult,
+            )
 
         def round_z(dst, gained, lost):
             nc.vector.tensor_tensor(
@@ -271,39 +288,48 @@ def tile_picked_advect_none_p_kernel(
             )
 
         z_grouped = [tile([P, w * PACK], BF16, "z_grouped%d" % c) for c, w in OUT_CHUNKS]
-        w3q = quantize(w3_grouped[:].rearrange("p c j -> p (c j)"), "w3")
-        low, high = slice(0, P), slice(P, 2 * P)
-
-        def add_on_gpsimd(n, gated):
-            lost = tile([P, TILES, P], F32, "lost%d" % n)[:]
-            nc.gpsimd.tensor_tensor(lost, gated, staying[:, n], ALU.add)
-            return lost
 
         def leave(n):
-            finish(n, w3q, quantize(z_grouped[n][:], "z%d" % n))
+            return multiply(n, w3q, quantize(z_grouped[n][:], "z%d" % n))
 
-        gated = tile([P, 2, TILES, P], F32, "w1p1_g")
-        lost = []
-        for n, part in enumerate((low, high)):
-            gate(gated[:, n], n, from_east[0][:, :, part], ALU.min)
-            lost.append(add_on_gpsimd(n, gated[:, n]))
-        gained = tile([P, 2, TILES, P], F32, "from_east0")
-        for n, part in enumerate((low, high)):
-            gate(gained[:, n], n, from_west[0][:, :, part], ALU.max)
+        stay(0)
+        stay(1)
+        w3q = quantize(w3_grouped[:].rearrange("p c j -> p (c j)"), "w3")
+        stay(2)
+        gated = tile([P, TILES, S // 2], F32, "w1p1_g")
+        lost = tile([P, TILES, S // 2], F32, "lost")
+        gate_east(gated[:, pairs[0], :], 0, 0)
+        add_staying(lost, gated[:, pairs[0], :], 0, 0)
+        stay(3)
+        gate_east(gated[:, pairs[1], :], 1, 0)
+        add_staying(lost, gated[:, pairs[1], :], 1, 0)
+        gained = tile([P, TILES, S // 2], F32, "from_east00")
+        for u in range(2):
+            gate_west(gained, u, 0)
+        gated_first = tile([P, 2, S // 2], F32, "from_west0_0")
+        gate_east(gated_first[:], 0, 1)
         for n in range(2):
-            round_z(z_grouped[0][:, n * P * PACK : (n + 1) * P * PACK], gained[:, n], lost[n])
-        gated = tile([P, 2, TILES, P], F32, "from_east0")
-        gate(gated[:, 0], 2, from_east[1][:, :, low], ALU.min)
-        lost = add_on_gpsimd(2, gated[:, 0])
-        leave(0)
-        gate(gated[:, 1], 3, from_east[1][:, :, high], ALU.min)
-        gained = tile([P, TILES, P], F32, "z_grouped0")[:]
-        gate(gained, 2, from_west[1][:], ALU.max)
-        round_z(z_grouped[1][:], gained, lost)
-        lost = tile([P, TILES, P], F32, "lost2")[:]
-        add_staying(lost, 3, gated[:, 1])
-        gained = tile([P, TILES, P], F32, "z_grouped0")[:]
-        gate(gained, 3, from_west[2][:], ALU.max)
-        leave(1)
-        round_z(z_grouped[2][:], gained, lost)
-        leave(2)
+            round_z(z_grouped[0][:, n * P * PACK : (n + 1) * P * PACK], gained[:, :, chunk(n)], lost[:, :, chunk(n)])
+        lost = tile([P, TILES, S // 2], F32, "from_east00")
+        add_staying(lost, gated_first[:], 0, 1)
+        late = tile([P, TILES + 2, S // 2], F32, "w1p1_g")
+        gained, gated_second = late[:, 0:TILES, :], late[:, TILES:, :]
+        gate_east(gated_second, 1, 1)
+        add_staying(lost, gated_second, 1, 1)
+        for u in range(2):
+            gate_west(gained, u, 1)
+        for h, part in enumerate(leave(0)):
+            store("scalar", nc.sync, "result0_%d" % h, *part)
+        for u in range(2):
+            gate_west(gained, u, 2)
+        round_z(z_grouped[1][:], gained[:, :, chunk(0)], lost[:, :, chunk(0)])
+        half_chunk = P // 2
+        parts = []
+        for first in (0, half_chunk):
+            cells = slice(P + first, P + first + half_chunk)
+            round_z(z_grouped[2][:, first * PACK : (first + half_chunk) * PACK], gained[:, :, cells], lost[:, :, cells])
+            parts.extend(leave(1 if first == 0 else 2))
+        store("scalar", nc.sync, "result1_0", *parts[0])
+        store("vector", nc.sync, "z_grouped384", *parts[1])
+        for h, part in enumerate(parts[2:]):
+            store("scalar" if h % 2 == 0 else "vector", nc.scalar if h == 2 else nc.sync, "result2_%d" % h, *part)

@@ -156,8 +156,8 @@ def tile_picked_advect_none_p_kernel(
         def chunk(n):
             return slice(n * P, (n + 1) * P)
 
-        def speeds_pass(wq, z, chunks):
-            codes, scales = wq
+        def speeds_pass(z, chunks):
+            codes, scales = w2q[z]
             for n in chunks:
                 nc.tensor.matmul_mx(
                     out=u_banks[n][:],
@@ -169,16 +169,16 @@ def tile_picked_advect_none_p_kernel(
                     stop=(z == PASSES - 1),
                 )
 
-        u_banks = [bank(n, [P, H]) for n in range(CHUNKS)]
-        w2q = quantize(round_pass([w2_raw[0][:]], "w2p0")[:].rearrange("p t c -> p (t c)"), "w2p0")
+        u_banks = [bank(n, [P, H]) for n in range(CHUNKS - 1)]
+        w2q = [quantize(round_pass([w2_raw[0][:]], "w2p0")[:].rearrange("p t c -> p (t c)"), "w2p0")]
         gather_words(0)
         nc.vector.tensor_copy(out=x_scale[:], in_=scale_table[:].indirect(offs_sb[:]))
-        speeds_pass(w2q, 0, range(CHUNKS))
-        w2q = quantize(round_pass([w2_raw[1][:]], "w2p1")[:].rearrange("p t c -> p (t c)"), "w2p1")
+        speeds_pass(0, range(CHUNKS - 1))
+        w2q.append(quantize(round_pass([w2_raw[1][:]], "w2p1")[:].rearrange("p t c -> p (t c)"), "w2p1"))
         x_codes.append(tile([P, S], U32, "w2p1_g"))
         for cells in WORD_PIECES:
             gather_words(1, cells)
-            speeds_pass(w2q, 1, range(cells.start // P, cells.stop // P))
+            speeds_pass(1, range(cells.start // P, min(cells.stop // P, CHUNKS - 1)))
         th_cells = [tile([P, H], F32, "th_cells%d" % n) for n in range(CHUNKS)]
         th = [[bank(CHUNKS + 2 * u + h, [P, 2, S // 2]) for h in range(2)] for u in range(2)]
         speed = tile([P, TILES, S], F32, "speed")
@@ -188,13 +188,17 @@ def tile_picked_advect_none_p_kernel(
                 nc.tensor.transpose(
                     th[t // 2][n // 2][:, t % 2, chunk(n % 2)], th_cells[n][:, t * P : (t + 1) * P], identity[:]
                 )
+            if n == 0:
+                u_banks.append(bank(0, [P, H]))
+                for z in range(PASSES):
+                    speeds_pass(z, [CHUNKS - 1])
         pairs = (slice(0, 2), slice(2, 4))
         halves = (slice(0, S // 2), slice(S // 2, S))
         for u in range(2):
             for h in range(2):
                 nc.scalar.activation(out=speed[:, pairs[u], halves[h]], in_=th[u][h][:], func=ACT.Abs, scale=0.5)
 
-        y_banks = [bank(t, [P, S]) for t in range(TILES)]
+        y_banks = [bank(index, [P, S]) for index in (3, 1, 2, 0)]
         w1q = quantize_pass((("vector", w1_raw[0][:]),), "w1p0", 4)
         for t in range(TILES):
             product(y_banks[t][:], w1q[t], 0)

@@ -172,8 +172,11 @@ def tile_picked_advect_none_p_kernel(
         u_banks = [bank(n, [P, H]) for n in range(CHUNKS - 1)]
         w2q = [quantize(round_pass([w2_raw[0][:]], "w2p0")[:].rearrange("p t c -> p (t c)"), "w2p0")]
         gather_words(0)
-        nc.vector.tensor_copy(out=x_scale[:], in_=scale_table[:].indirect(offs_sb[:]))
-        speeds_pass(0, range(CHUNKS - 1))
+        for h in range(2):
+            cells = slice(h * S // 2, (h + 1) * S // 2)
+            offsets = offs_sb[:, cells.start // 16 : cells.stop // 16]
+            nc.vector.tensor_copy(out=x_scale[:, cells], in_=scale_table[:].indirect(offsets))
+            speeds_pass(0, range(2 * h, min(2 * h + 2, CHUNKS - 1)))
         w2q.append(quantize(round_pass([w2_raw[1][:]], "w2p1")[:].rearrange("p t c -> p (t c)"), "w2p1"))
         x_codes.append(tile([P, S], U32, "w2p1_g"))
         for cells in WORD_PIECES:
@@ -184,14 +187,14 @@ def tile_picked_advect_none_p_kernel(
         speed = tile([P, TILES, S], F32, "speed")
         for n in range(CHUNKS):
             nc.scalar.activation(out=th_cells[n][:], in_=u_banks[n][:], func=ACT.Tanh)
-            for t in range(TILES):
-                nc.tensor.transpose(
-                    th[t // 2][n // 2][:, t % 2, chunk(n % 2)], th_cells[n][:, t * P : (t + 1) * P], identity[:]
-                )
             if n == 0:
                 u_banks.append(bank(0, [P, H]))
                 for z in range(PASSES):
                     speeds_pass(z, [CHUNKS - 1])
+            for t in range(TILES):
+                nc.tensor.transpose(
+                    th[t // 2][n // 2][:, t % 2, chunk(n % 2)], th_cells[n][:, t * P : (t + 1) * P], identity[:]
+                )
         pairs = (slice(0, 2), slice(2, 4))
         halves = (slice(0, S // 2), slice(S // 2, S))
         for u in range(2):
@@ -199,7 +202,7 @@ def tile_picked_advect_none_p_kernel(
                 nc.scalar.activation(out=speed[:, pairs[u], halves[h]], in_=th[u][h][:], func=ACT.Abs, scale=0.5)
 
         y_banks = [bank(index, [P, S]) for index in (3, 1, 2, 0)]
-        w1q = quantize_pass((("vector", w1_raw[0][:]),), "w1p0", 4)
+        w1q = quantize_pass((("vector", w1_raw[0][:]),), "w1p0", 2)
         for t in range(TILES):
             product(y_banks[t][:], w1q[t], 0)
         w1q = quantize_pass((("vector", w1_raw[1][0][:]), ("vector", w1_raw[1][1][:])), "w1p1", 1)
@@ -319,7 +322,7 @@ def tile_picked_advect_none_p_kernel(
         late = tile([P, TILES + 2, S // 2], F32, "w1p1_g")
         gained, gated_second = late[:, 0:TILES, :], late[:, TILES:, :]
         gate_east(gated_second, 1, 1)
-        add_staying(lost, gated_second, 1, 1)
+        nc.gpsimd.tensor_tensor(lost[:, pairs[1], chunk(0)], gated_second[:, :, chunk(0)], staying[:, pairs[1], chunk(2)], ALU.add)
         for u in range(2):
             gate_west(gained, u, 1)
         for h, part in enumerate(leave(0)):
@@ -327,12 +330,10 @@ def tile_picked_advect_none_p_kernel(
         for u in range(2):
             gate_west(gained, u, 2)
         round_z(z_grouped[1][:], gained[:, :, chunk(0)], lost[:, :, chunk(0)])
-        half_chunk = P // 2
-        parts = []
-        for first in (0, half_chunk):
-            cells = slice(P + first, P + first + half_chunk)
-            round_z(z_grouped[2][:, first * PACK : (first + half_chunk) * PACK], gained[:, :, cells], lost[:, :, cells])
-            parts.extend(leave(1 if first == 0 else 2))
+        nc.vector.tensor_tensor(lost[:, pairs[1], chunk(1)], gated_second[:, :, chunk(1)], staying[:, pairs[1], chunk(3)], ALU.add)
+        parts = leave(1)
+        round_z(z_grouped[2][:], gained[:, :, chunk(1)], lost[:, :, chunk(1)])
+        parts.extend(leave(2))
         store("scalar", nc.sync, "result1_0", *parts[0])
         store("vector", nc.sync, "z_grouped384", *parts[1])
         for h, part in enumerate(parts[2:]):

@@ -32,10 +32,14 @@ def tile_picked_advect_none_p_kernel(
     nc = tc.nc
     with ExitStack() as ctx:
         sb = ctx.enter_context(tc.tile_pool(name="sb", bufs=1))
+        shared = ctx.enter_context(tc.tile_pool(name="shared", bufs=1))
         psum = ctx.enter_context(tc.psum_pool(name="psum", bufs=1))
 
         def tile(shape, dtype, name):
             return sb.tile(shape, dtype, name=name, align_bytes=64)
+
+        def placed(shape, name, first_column):
+            return shared.tile(shape, F32, name=name, align_bytes=64, offset=4 * first_column)
 
         def bank(index, shape):
             return psum.tile(shape, F32, name="bank%d" % index)
@@ -56,8 +60,7 @@ def tile_picked_advect_none_p_kernel(
                 out=word_table[z][:], in_=x_words[z].rearrange("p c r -> p (c r)").bitcast(I32)
             )
 
-        def load_rows(w, z, name):
-            raw = tile([P, PACK, H], F32, name)
+        def load_rows(w, z, raw):
             nc.sync.dma_start(
                 out=raw[:], in_=w[z * K_PASS : (z + 1) * K_PASS, :].rearrange("(p j) c -> p j c", j=PACK)
             )
@@ -80,17 +83,17 @@ def tile_picked_advect_none_p_kernel(
                         in_=x_scales[z, r : 16 : 4, :].bitcast(I32),
                     )
 
-        w2_raw = [load_rows(w2, 0, "w2_raw0")]
+        w2_raw = [load_rows(w2, 0, tile([P, PACK, H], F32, "w2_raw0"))]
         nc.sync.dma_start(offs_sb[:], offs)
         load_scale_rows(range(0, 2))
         load_words(0)
         load_scale_rows(range(2, 4))
-        w2_raw.append(load_rows(w2, 1, "w2_raw1"))
+        w2_raw.append(load_rows(w2, 1, tile([P, PACK, H], F32, "w2_raw1")))
         load_words(1)
-        w1_raw = [load_rows(w1, 0, "w1_raw0"), load_parts(w1, 1, "w1_raw1")]
-        w3_all = load_rows(w3, 0, "w3_all")
+        w1_raw = [load_rows(w1, 0, tile([P, PACK, H], F32, "w1_raw0")), load_parts(w1, 1, "w1_raw1")]
         nc.sync.dma_start(east_sb[:], east)
         nc.sync.dma_start(west_sb[:], west)
+        w3_all = load_rows(w3, 0, placed([P, PACK, N], "w3_all", 0))
 
         def copy_on(engine, dst, src):
             if engine == "vector":
@@ -205,9 +208,16 @@ def tile_picked_advect_none_p_kernel(
         w1q = quantize_pass((("vector", w1_raw[0][:]),), "w1p0", 2)
         for t in range(TILES):
             product(y_banks[t][:], w1q[t], 0)
-        w1q = quantize_pass((("vector", w1_raw[1][0][:]), ("vector", w1_raw[1][1][:])), "w1p1", 1)
+        grouped = tile([P, TILES, K_PASS], BF16, "w1p1_g")
+        cast("vector", grouped, 0, w1_raw[1][0][:])
+        for pair in pairs:
+            nc.vector.tensor_copy(
+                out=grouped[:, pair, H // 2 :].rearrange("p t (m j) -> p m j t", j=PACK),
+                in_=w1_raw[1][1][:].rearrange("p j (m t) -> p m j t", t=TILES)[:, :, :, pair],
+            )
         for t in range(TILES):
-            product(y_banks[t][:], w1q[t], 1)
+            codes, scales = quantize(grouped[:, t, :], "w1p1_%d" % t)
+            product(y_banks[t][:], (codes[:], scales[:]), 1)
 
         w3_grouped = tile([P, N, PACK], BF16, "w1p1_g")
         nc.gpsimd.tensor_scalar(w3_grouped[:], w3_all[:].rearrange("p j c -> p c j"), 1.0, 0.0, ALU.mult, ALU.add)
@@ -263,16 +273,16 @@ def tile_picked_advect_none_p_kernel(
             copy_on(engine, result[:], acc[:])
             queue.dma_start(out=dst, in_=result[:])
 
-        staying = tile([P, TILES, S], F32, "staying")
+        staying = [tile([P, 2, S], F32, "staying")[:]]
 
         def stay(t):
-            nc.vector.scalar_tensor_tensor(staying[:, t, :], speed[:, t, :], 1.0, y_banks[t][:], ALU.subtract, ALU.mult)
+            nc.vector.scalar_tensor_tensor(staying[t // 2][:, t % 2, :], speed[:, t, :], 1.0, y_banks[t][:], ALU.subtract, ALU.mult)
 
         def gate_east(gated, u, h):
             nc.vector.scalar_tensor_tensor(gated, th[u][h][:], 0.0, from_east[u][h][:], ALU.min, ALU.mult)
 
         def add_staying(lost, gated, u, h):
-            nc.gpsimd.tensor_tensor(lost[:, pairs[u], :], gated, staying[:, pairs[u], halves[h]], ALU.add)
+            nc.gpsimd.tensor_tensor(lost[:, pairs[u], :], gated, staying[u][:, :, halves[h]], ALU.add)
 
         def gate_west(dst, u, n):
             c0, width = OUT_CHUNKS[n]
@@ -301,15 +311,17 @@ def tile_picked_advect_none_p_kernel(
 
         stay(0)
         stay(1)
+        gated = tile([P, 2, S // 2], F32, "gated")
+        gate_east(gated[:], 0, 0)
         w3q = quantize(w3_grouped[:].rearrange("p c j -> p (c j)"), "w3")
+        lost = tile([P, TILES, S // 2], F32, "w1p1_g")
+        staying.append(placed([P, 2, S], "staying_second", 0)[:])
+        add_staying(lost, gated[:], 0, 0)
         stay(2)
-        gated = tile([P, TILES, S // 2], F32, "w1p1_g")
-        lost = tile([P, TILES, S // 2], F32, "lost")
-        gate_east(gated[:, pairs[0], :], 0, 0)
-        add_staying(lost, gated[:, pairs[0], :], 0, 0)
         stay(3)
-        gate_east(gated[:, pairs[1], :], 1, 0)
-        add_staying(lost, gated[:, pairs[1], :], 1, 0)
+        gated = placed([P, 2, S // 2], "gated_second_pair", 2 * S)
+        gate_east(gated[:], 1, 0)
+        add_staying(lost, gated[:], 1, 0)
         gained = tile([P, TILES, S // 2], F32, "from_east00")
         for u in range(2):
             gate_west(gained, u, 0)
@@ -319,10 +331,10 @@ def tile_picked_advect_none_p_kernel(
             round_z(z_grouped[0][:, n * P * PACK : (n + 1) * P * PACK], gained[:, :, chunk(n)], lost[:, :, chunk(n)])
         lost = tile([P, TILES, S // 2], F32, "from_east00")
         add_staying(lost, gated_first[:], 0, 1)
-        late = tile([P, TILES + 2, S // 2], F32, "w1p1_g")
+        late = placed([P, TILES + 2, S // 2], "late", 2 * S)
         gained, gated_second = late[:, 0:TILES, :], late[:, TILES:, :]
         gate_east(gated_second, 1, 1)
-        nc.gpsimd.tensor_tensor(lost[:, pairs[1], chunk(0)], gated_second[:, :, chunk(0)], staying[:, pairs[1], chunk(2)], ALU.add)
+        nc.gpsimd.tensor_tensor(lost[:, pairs[1], chunk(0)], gated_second[:, :, chunk(0)], staying[1][:, :, chunk(2)], ALU.add)
         for u in range(2):
             gate_west(gained, u, 1)
         for h, part in enumerate(leave(0)):
@@ -330,7 +342,7 @@ def tile_picked_advect_none_p_kernel(
         for u in range(2):
             gate_west(gained, u, 2)
         round_z(z_grouped[1][:], gained[:, :, chunk(0)], lost[:, :, chunk(0)])
-        nc.vector.tensor_tensor(lost[:, pairs[1], chunk(1)], gated_second[:, :, chunk(1)], staying[:, pairs[1], chunk(3)], ALU.add)
+        nc.vector.tensor_tensor(lost[:, pairs[1], chunk(1)], gated_second[:, :, chunk(1)], staying[1][:, :, chunk(3)], ALU.add)
         parts = leave(1)
         round_z(z_grouped[2][:], gained[:, :, chunk(1)], lost[:, :, chunk(1)])
         parts.extend(leave(2))

@@ -23,6 +23,7 @@ PASSES = K // K_PASS
 TILES = H // P
 CHUNKS = S // P
 OUT_CHUNKS = ((0, 256), (256, 128), (384, 128))
+WEST_PIECES = (((0, 256), (256, 256)), OUT_CHUNKS)
 WORD_PIECES = (slice(0, 128), slice(128, 256), slice(256, 512))
 
 
@@ -224,7 +225,7 @@ def tile_picked_advect_none_p_kernel(
 
         half = [tile([P, S], F32, "half%d" % t) for t in range(TILES)]
         from_east = [[tile([P, 2, S // 2], F32, "from_east%d%d" % (u, h)) for h in range(2)] for u in range(2)]
-        from_west = [[tile([P, 2, w], F32, "from_west%d_%d" % (u, c)) for c, w in OUT_CHUNKS] for u in range(2)]
+        from_west = [[tile([P, 2, w], F32, "from_west%d_%d" % (u, c)) for c, w in WEST_PIECES[u]] for u in range(2)]
 
         def fetch(terms, lists, u, c0):
             for n in range(2):
@@ -239,9 +240,9 @@ def tile_picked_advect_none_p_kernel(
             fetch(from_west[u][0], west_sb, u, 0)
         for u in range(2):
             fetch(from_east[u][1], east_sb, u, S // 2)
-        for n in range(1, 3):
-            for u in range(2):
-                fetch(from_west[u][n], west_sb, u, OUT_CHUNKS[n][0])
+        for u in range(2):
+            for n in range(1, len(WEST_PIECES[u])):
+                fetch(from_west[u][n], west_sb, u, WEST_PIECES[u][n][0])
 
         out_view = out.rearrange("(mt p) c -> p mt c", p=P)
         out_banks = ((0, 1), (2, 3), (4, 6, 5, 7))
@@ -285,7 +286,7 @@ def tile_picked_advect_none_p_kernel(
             nc.gpsimd.tensor_tensor(lost[:, pairs[u], :], gated, staying[u][:, :, halves[h]], ALU.add)
 
         def gate_west(dst, u, n):
-            c0, width = OUT_CHUNKS[n]
+            c0, width = WEST_PIECES[u][n]
             first = c0 % (S // 2)
             nc.vector.scalar_tensor_tensor(
                 dst[:, pairs[u], first : first + width],
@@ -329,18 +330,28 @@ def tile_picked_advect_none_p_kernel(
         gate_east(gated_first[:], 0, 1)
         for n in range(2):
             round_z(z_grouped[0][:, n * P * PACK : (n + 1) * P * PACK], gained[:, :, chunk(n)], lost[:, :, chunk(n)])
+        z_first = (tile([P, 2 * P], U32, "z0_codes"), tile([P, 2 * P], U8, "z0_scales"))
+
+        def quantize_first(n):
+            nc.vector.quantize_mx(
+                out=z_first[0][:, chunk(n)].bitcast(FP8X4),
+                scales=z_first[1][:, chunk(n)],
+                in_=z_grouped[0][:, n * P * PACK : (n + 1) * P * PACK],
+            )
+
+        quantize_first(0)
         lost = tile([P, TILES, S // 2], F32, "from_east00")
         add_staying(lost, gated_first[:], 0, 1)
         late = placed([P, TILES + 2, S // 2], "late", 2 * S)
         gained, gated_second = late[:, 0:TILES, :], late[:, TILES:, :]
         gate_east(gated_second, 1, 1)
         nc.gpsimd.tensor_tensor(lost[:, pairs[1], chunk(0)], gated_second[:, :, chunk(0)], staying[1][:, :, chunk(2)], ALU.add)
-        for u in range(2):
-            gate_west(gained, u, 1)
-        for h, part in enumerate(leave(0)):
+        gate_west(gained, 0, 1)
+        quantize_first(1)
+        for h, part in enumerate(multiply(0, w3q, z_first)):
             store("scalar", nc.sync, "result0_%d" % h, *part)
-        for u in range(2):
-            gate_west(gained, u, 2)
+        for n in range(1, 3):
+            gate_west(gained, 1, n)
         round_z(z_grouped[1][:], gained[:, :, chunk(0)], lost[:, :, chunk(0)])
         nc.vector.tensor_tensor(lost[:, pairs[1], chunk(1)], gated_second[:, :, chunk(1)], staying[1][:, :, chunk(3)], ALU.add)
         parts = leave(1)

from contextlib import ExitStack

import concourse.mybir as mybir
from concourse.masks import make_identity

K, T, S, N, H = 1024, 2048, 512, 512, 512
FLOPS = 2 * (2 * K * H * S + H * N * S)

F32 = mybir.dt.float32
BF16 = mybir.dt.bfloat16
I32 = mybir.dt.int32
U32 = mybir.dt.uint32
U16 = mybir.dt.uint16
U8 = mybir.dt.uint8
FP8X4 = mybir.dt.float8_e4m3fn_x4
ALU = mybir.AluOpType
ACT = mybir.ActivationFunctionType

P = 128
PACK = 4
K_PASS = P * PACK
PASSES = K // K_PASS
TILES = H // P
CHUNKS = S // P
OUT_CHUNKS = ((0, 256), (256, 128), (384, 128))
WEST_PIECES = (((0, 256), (256, 256)), OUT_CHUNKS)
WORD_PIECES = (slice(0, 128), slice(128, 256), slice(256, 512))


def tile_picked_advect_none_p_kernel(
    tc, x_words, x_scales, w1, w2, w3, offs, east, west, out
):
    nc = tc.nc
    with ExitStack() as ctx:
        sb = ctx.enter_context(tc.tile_pool(name="sb", bufs=1))
        shared = ctx.enter_context(tc.tile_pool(name="shared", bufs=1))
        psum = ctx.enter_context(tc.psum_pool(name="psum", bufs=1))

        def tile(shape, dtype, name):
            return sb.tile(shape, dtype, name=name, align_bytes=64)

        def placed(shape, name, first_column):
            return shared.tile(shape, F32, name=name, align_bytes=64, offset=4 * first_column)

        def bank(index, shape):
            return psum.tile(shape, F32, name="bank%d" % index)

        offs_sb = sb.tile([P, S // 16], U16, name="offs_sb")
        west_sb = sb.tile([P, S // 16], U16, name="west_sb")
        east_sb = sb.tile([P, S // 16], U16, name="east_sb")
        scale_table = tile([P, T], U8, "scale_table")
        nc.gpsimd.memset(scale_table[:].bitcast(I32), 0)

        identity = tile([P, P], F32, "identity")
        make_identity(nc, identity[:])

        word_table = [tile([P, T], I32, "word_table%d" % z) for z in range(PASSES)]

        def load_words(z):
            nc.sync.dma_start(
                out=word_table[z][:], in_=x_words[z].rearrange("p c r -> p (c r)").bitcast(I32)
            )

        def load_rows(w, z, raw):
            nc.sync.dma_start(
                out=raw[:], in_=w[z * K_PASS : (z + 1) * K_PASS, :].rearrange("(p j) c -> p j c", j=PACK)
            )
            return raw

        def load_parts(w, z, name, widths=(H // 2, H // 2)):
            rows = w[z * K_PASS : (z + 1) * K_PASS, :].rearrange("(p j) c -> p j c", j=PACK)
            parts, first = [], 0
            for h, width in enumerate(widths):
                parts.append(tile([P, PACK, width], F32, "%s_%d" % (name, h)))
                nc.sync.dma_start(out=parts[h][:], in_=rows[:, :, first : first + width])
                first = first + width
            return parts

        def load_scale_rows(rows):
            for r in rows:
                for z in range(PASSES):
                    nc.sync.dma_start(
                        out=scale_table[4 * z + r : P : 32, :].bitcast(I32),
                        in_=x_scales[z, r : 16 : 4, :].bitcast(I32),
                    )

        w2_raw = [load_rows(w2, 0, tile([P, PACK, H], F32, "w2_raw0"))]
        nc.sync.dma_start(offs_sb[:], offs)
        load_scale_rows(range(0, 2))
        load_words(0)
        load_scale_rows(range(2, 4))
        w2_raw.append(load_rows(w2, 1, tile([P, PACK, H], F32, "w2_raw1")))
        load_words(1)
        w1_raw = [load_rows(w1, 0, tile([P, PACK, H], F32, "w1_raw0")), load_parts(w1, 1, "w1_raw1")]
        nc.sync.dma_start(east_sb[:], east)
        nc.sync.dma_start(west_sb[:], west)
        w3_all = load_rows(w3, 0, placed([P, PACK, N], "w3_all", 0))

        def copy_on(engine, dst, src):
            if engine == "vector":
                nc.vector.tensor_copy(out=dst, in_=src)
            else:
                nc.scalar.copy(out=dst, in_=src)

        def cast(engine, grouped, first, raw):
            copy_on(
                engine,
                grouped[:, :, first : first + raw.shape[2]].rearrange("p t (m j) -> p m j t", j=PACK),
                raw.rearrange("p j (m t) -> p m j t", t=TILES),
            )

        def quantize(grouped, name):
            width = grouped.shape[1] // PACK
            codes = tile([P, width], U32, name + "_codes")
            scales = tile([P, width], U8, name + "_scales")
            nc.vector.quantize_mx(out=codes[:].bitcast(FP8X4), scales=scales[:], in_=grouped)
            return codes, scales

        def quantize_pass(shares, name, tiles_a_call):
            grouped = tile([P, TILES, K_PASS], BF16, name + "_g")
            first = 0
            for engine, raw in shares:
                cast(engine, grouped, first, raw)
                first = first + raw.shape[2]
            pairs = []
            for t in range(0, TILES, tiles_a_call):
                rows = grouped[:, t : t + tiles_a_call, :].rearrange("p t c -> p (t c)")
                codes, scales = quantize(rows, "%s_%d" % (name, t))
                for u in range(tiles_a_call):
                    pairs.append((codes[:, u * P : (u + 1) * P], scales[:, u * P : (u + 1) * P]))
            return pairs

        x_codes = [tile([P, S], U32, "x_codes0")]
        x_scale = tile([P, S], U8, "x_scale")

        def gather_words(z, cells=slice(0, S)):
            offsets = offs_sb[:, cells.start // 16 : cells.stop // 16]
            nc.vector.tensor_copy(out=x_codes[z][:, cells], in_=word_table[z][:].bitcast(U32).indirect(offsets))

        def product(acc, wq, z, cells=slice(0, S), opens=True, closes=True):
            codes, scales = wq
            nc.tensor.matmul_mx(
                out=acc,
                lhsT=codes.bitcast(FP8X4),
                lhsT_scale=scales,
                rhs=x_codes[z][:, cells].bitcast(FP8X4),
                rhs_scale=x_scale[4 * z : P, cells],
                start=(z == 0 and opens),
                stop=(z == PASSES - 1 and closes),
            )

        def round_pass(raws, name):
            grouped = tile([P, TILES, K_PASS], BF16, name + "_g")
            first = 0
            for raw in raws:
                cast("vector", grouped, first, raw)
                first = first + raw.shape[2]
            return grouped

        def chunk(n):
            return slice(n * P, (n + 1) * P)

        def speeds_pass(z, chunks):
            codes, scales = w2q[z]
            for n in chunks:
                nc.tensor.matmul_mx(
                    out=u_banks[n][:],
                    lhsT=x_codes[z][:, chunk(n)].bitcast(FP8X4),
                    lhsT_scale=x_scale[4 * z : P, chunk(n)],
                    rhs=codes[:].bitcast(FP8X4),
                    rhs_scale=scales[:],
                    start=(z == 0),
                    stop=(z == PASSES - 1),
                )

        u_banks = [bank(n, [P, H]) for n in range(CHUNKS - 1)]
        w2q = [quantize(round_pass([w2_raw[0][:]], "w2p0")[:].rearrange("p t c -> p (t c)"), "w2p0")]
        gather_words(0)
        for h in range(2):
            cells = slice(h * S // 2, (h + 1) * S // 2)
            offsets = offs_sb[:, cells.start // 16 : cells.stop // 16]
            nc.vector.tensor_copy(out=x_scale[:, cells], in_=scale_table[:].indirect(offsets))
            speeds_pass(0, range(2 * h, min(2 * h + 2, CHUNKS - 1)))
        w2q.append(quantize(round_pass([w2_raw[1][:]], "w2p1")[:].rearrange("p t c -> p (t c)"), "w2p1"))
        x_codes.append(tile([P, S], U32, "w2p1_g"))
        for cells in WORD_PIECES:
            gather_words(1, cells)
            speeds_pass(1, range(cells.start // P, min(cells.stop // P, CHUNKS - 1)))
        th_cells = [tile([P, H], F32, "th_cells%d" % n) for n in range(CHUNKS)]
        th = [[bank(CHUNKS + 2 * u + h, [P, 2, S // 2]) for h in range(2)] for u in range(2)]
        speed = tile([P, TILES, S], F32, "speed")
        for n in range(CHUNKS):
            nc.scalar.activation(out=th_cells[n][:], in_=u_banks[n][:], func=ACT.Tanh)
            if n == 0:
                u_banks.append(bank(0, [P, H]))
                for z in range(PASSES):
                    speeds_pass(z, [CHUNKS - 1])
            for t in range(TILES):
                nc.tensor.transpose(
                    th[t // 2][n // 2][:, t % 2, chunk(n % 2)], th_cells[n][:, t * P : (t + 1) * P], identity[:]
                )
        pairs = (slice(0, 2), slice(2, 4))
        halves = (slice(0, S // 2), slice(S // 2, S))
        for u in range(2):
            for h in range(2):
                nc.scalar.activation(out=speed[:, pairs[u], halves[h]], in_=th[u][h][:], func=ACT.Abs, scale=0.5)

        y_banks = [bank(index, [P, S]) for index in (3, 1, 2, 0)]
        w1q = quantize_pass((("vector", w1_raw[0][:]),), "w1p0", 2)
        for t in range(TILES):
            product(y_banks[t][:], w1q[t], 0)
        grouped = tile([P, TILES, K_PASS], BF16, "w1p1_g")
        cast("vector", grouped, 0, w1_raw[1][0][:])
        for pair in pairs:
            nc.vector.tensor_copy(
                out=grouped[:, pair, H // 2 :].rearrange("p t (m j) -> p m j t", j=PACK),
                in_=w1_raw[1][1][:].rearrange("p j (m t) -> p m j t", t=TILES)[:, :, :, pair],
            )
        for t in range(TILES):
            codes, scales = quantize(grouped[:, t, :], "w1p1_%d" % t)
            product(y_banks[t][:], (codes[:], scales[:]), 1)

        w3_grouped = tile([P, N, PACK], BF16, "w1p1_g")
        nc.gpsimd.tensor_scalar(w3_grouped[:], w3_all[:].rearrange("p j c -> p c j"), 1.0, 0.0, ALU.mult, ALU.add)

        half = [tile([P, S], F32, "half%d" % t) for t in range(TILES)]
        from_east = [[tile([P, 2, S // 2], F32, "from_east%d%d" % (u, h)) for h in range(2)] for u in range(2)]
        from_west = [[tile([P, 2, w], F32, "from_west%d_%d" % (u, c)) for c, w in WEST_PIECES[u]] for u in range(2)]

        def fetch(terms, lists, u, c0):
            for n in range(2):
                offsets = lists[:, c0 // 16 : (c0 + terms.shape[2]) // 16]
                nc.scalar.activation(out=terms[:, n, :], in_=half[2 * u + n][:].indirect(offsets), func=ACT.Copy)

        nc.scalar.activation(out=half[0][:], in_=y_banks[0][:], func=ACT.Copy, scale=0.5)
        for t in range(1, TILES):
            nc.vector.tensor_scalar_mul(half[t][:], y_banks[t][:], 0.5)
        for u in range(2):
            fetch(from_east[u][0], east_sb, u, 0)
            fetch(from_west[u][0], west_sb, u, 0)
        for u in range(2):
            fetch(from_east[u][1], east_sb, u, S // 2)
        for u in range(2):
            for n in range(1, len(WEST_PIECES[u])):
                fetch(from_west[u][n], west_sb, u, WEST_PIECES[u][n][0])

        out_view = out.rearrange("(mt p) c -> p mt c", p=P)
        out_banks = ((0, 1), (2, 3), (4, 6, 5, 7))

        def multiply(n, w3q, zq):
            (w3_codes, w3_scales), (z_codes, z_scales) = w3q, zq
            c0, width = OUT_CHUNKS[n]
            cols = slice(c0, c0 + width)
            rows = TILES // len(out_banks[n])
            accs = []
            for h, index in enumerate(out_banks[n]):
                acc = bank(index, [P, rows, width])
                accs.append((acc, out_view[:, rows * h : rows * (h + 1), cols]))
                for m in range(rows):
                    mt = rows * h + m
                    nc.tensor.matmul_mx(
                        out=acc[:, m, :],
                        lhsT=w3_codes[:, mt * P : (mt + 1) * P].bitcast(FP8X4),
                        lhsT_scale=w3_scales[:, mt * P : (mt + 1) * P],
                        rhs=z_codes[:].bitcast(FP8X4),
                        rhs_scale=z_scales[:],
                        start=True,
                        stop=True,
                    )
            return accs

        def store(engine, queue, name, acc, dst):
            result = tile(list(acc.shape), F32, name)
            copy_on(engine, result[:], acc[:])
            queue.dma_start(out=dst, in_=result[:])

        staying = [tile([P, 2, S], F32, "staying")[:]]

        def stay(t):
            nc.vector.scalar_tensor_tensor(staying[t // 2][:, t % 2, :], speed[:, t, :], 1.0, y_banks[t][:], ALU.subtract, ALU.mult)

        def gate_east(gated, u, h):
            nc.vector.scalar_tensor_tensor(gated, th[u][h][:], 0.0, from_east[u][h][:], ALU.min, ALU.mult)

        def add_staying(lost, gated, u, h):
            nc.gpsimd.tensor_tensor(lost[:, pairs[u], :], gated, staying[u][:, :, halves[h]], ALU.add)

        def gate_west(dst, u, n):
            c0, width = WEST_PIECES[u][n]
            first = c0 % (S // 2)
            nc.vector.scalar_tensor_tensor(
                dst[:, pairs[u], first : first + width],
                th[u][c0 // (S // 2)][:, :, first : first + width],
                0.0,
                from_west[u][n][:],
                ALU.max,
                ALU.mult,
            )

        def round_z(dst, gained, lost):
            nc.vector.tensor_tensor(
                dst.rearrange("p (c i t) -> p c t i", i=2, t=TILES),
                gained.rearrange("p t (c i) -> p c t i", i=2),
                lost.rearrange("p t (c i) -> p c t i", i=2),
                ALU.subtract,
            )

        z_grouped = [tile([P, w * PACK], BF16, "z_grouped%d" % c) for c, w in OUT_CHUNKS]

        def leave(n):
            return multiply(n, w3q, quantize(z_grouped[n][:], "z%d" % n))

        stay(0)
        stay(1)
        gated = tile([P, 2, S // 2], F32, "gated")
        gate_east(gated[:], 0, 0)
        w3q = quantize(w3_grouped[:].rearrange("p c j -> p (c j)"), "w3")
        lost = tile([P, TILES, S // 2], F32, "w1p1_g")
        staying.append(placed([P, 2, S], "staying_second", 0)[:])
        add_staying(lost, gated[:], 0, 0)
        stay(2)
        stay(3)
        gated = placed([P, 2, S // 2], "gated_second_pair", 2 * S)
        gate_east(gated[:], 1, 0)
        add_staying(lost, gated[:], 1, 0)
        gained = tile([P, TILES, S // 2], F32, "from_east00")
        for u in range(2):
            gate_west(gained, u, 0)
        gated_first = tile([P, 2, S // 2], F32, "from_west0_0")
        gate_east(gated_first[:], 0, 1)
        for n in range(2):
            round_z(z_grouped[0][:, n * P * PACK : (n + 1) * P * PACK], gained[:, :, chunk(n)], lost[:, :, chunk(n)])
        z_first = (tile([P, 2 * P], U32, "z0_codes"), tile([P, 2 * P], U8, "z0_scales"))

        def quantize_first(n):
            nc.vector.quantize_mx(
                out=z_first[0][:, chunk(n)].bitcast(FP8X4),
                scales=z_first[1][:, chunk(n)],
                in_=z_grouped[0][:, n * P * PACK : (n + 1) * P * PACK],
            )

        quantize_first(0)
        lost = tile([P, TILES, S // 2], F32, "from_east00")
        add_staying(lost, gated_first[:], 0, 1)
        late = placed([P, TILES + 2, S // 2], "late", 2 * S)
        gained, gated_second = late[:, 0:TILES, :], late[:, TILES:, :]
        gate_east(gated_second, 1, 1)
        nc.gpsimd.tensor_tensor(lost[:, pairs[1], chunk(0)], gated_second[:, :, chunk(0)], staying[1][:, :, chunk(2)], ALU.add)
        gate_west(gained, 0, 1)
        quantize_first(1)
        for h, part in enumerate(multiply(0, w3q, z_first)):
            store("scalar", nc.sync, "result0_%d" % h, *part)
        for n in range(1, 3):
            gate_west(gained, 1, n)
        round_z(z_grouped[1][:], gained[:, :, chunk(0)], lost[:, :, chunk(0)])
        nc.vector.tensor_tensor(lost[:, pairs[1], chunk(1)], gated_second[:, :, chunk(1)], staying[1][:, :, chunk(3)], ALU.add)
        parts = leave(1)
        round_z(z_grouped[2][:], gained[:, :, chunk(1)], lost[:, :, chunk(1)])
        parts.extend(leave(2))
        store("scalar", nc.sync, "result1_0", *parts[0])
        store("vector", nc.sync, "z_grouped384", *parts[1])
        for h, part in enumerate(parts[2:]):
            store("scalar" if h % 2 == 0 else "vector", nc.scalar if h == 2 else nc.sync, "result2_%d" % h, *part)
